import numpy as np
import ml_dtypes


def mxq(x, axis, fmt="e4m3"):
    dtype, down = {"e4m3": (ml_dtypes.float8_e4m3fn, 7), "e5m2": (ml_dtypes.float8_e5m2, 14)}[fmt]
    v = np.moveaxis(np.asarray(x, np.float32).astype(ml_dtypes.bfloat16).astype(np.float64), axis, -1)
    blocks = v.reshape(v.shape[:-1] + (-1, 32))
    amax = np.abs(blocks).max(-1, keepdims=True)
    byte = np.maximum(np.where(amax > 0, np.frexp(amax)[1] - 1 + 127, 0) - down, 1)
    scale = np.exp2(byte - 127.0)
    codes = (blocks / scale).astype(np.float32).astype(dtype).astype(np.float64)
    return np.moveaxis((codes * scale).reshape(v.shape), -1, axis)


WIDE = False


def mx_kscale(k):
    if not WIDE:
        return np.ones(k)
    levels = np.array([10, -10, 5, -5, 0])
    if k % 512:
        return np.exp2(np.random.permutation(np.resize(levels, k // 32))).repeat(32)
    a = np.empty((k // 512, 16))
    for p in range(k // 512):
        a[p, :8] = np.random.permutation(np.resize(levels, 8))
        for g in range(8):
            far = levels[np.abs(levels - a[p, g]) >= 10]
            a[p, g + 8] = far[np.random.randint(len(far))]
    return np.exp2(a.ravel()).repeat(32)


BF16 = ml_dtypes.bfloat16


def bf(x):
    return np.asarray(x, np.float32).astype(BF16)


def f64(x):
    return np.asarray(x).astype(np.float64)


B, F, D, A, O = 512, 8, 512, 512, 1024


def pair_products(v):
    blocks = []
    for i in range(F - 1):
        blocks.append(v[:, i:i + 1, :] * v[:, i + 1:, :])
    return np.concatenate(blocks, axis=1)


def draw0():
    s, t = mx_kscale(D), mx_kscale(D)
    return {
        "v": bf(np.random.standard_normal((B, F, D))),
        "ga": bf((1.0 + 0.1 * np.random.standard_normal(D)) * s),
        "wa": bf(np.random.standard_normal((D, A)) / np.sqrt(D) / s[:, None]),
        "ba": bf(0.5 * np.random.standard_normal(A)),
        "h": bf(2.0 * np.random.standard_normal(A) / np.sqrt(A)),
        "gp": bf((1.0 + 0.1 * np.random.standard_normal(D)) * t),
        "wp": bf(3.0 * np.random.standard_normal((D, O)) / np.sqrt(D) / t[:, None]),
    }


def core(v, ga, wa, ba, h, gp, wp):
    e = pair_products(f64(v))
    eg = e * f64(ga)[None, None, :]
    z = np.maximum((mxq(eg, 2, "e4m3") @ mxq(f64(wa), 0, "e4m3")) + f64(ba)[None, None, :], 0.0)
    sc = np.sum(z * f64(h)[None, None, :], axis=2)
    p = np.exp(sc - np.max(sc, axis=1, keepdims=True))
    al = p / np.sum(p, axis=1, keepdims=True)
    pool = f64(gp)[None, :] * np.sum(al[:, :, None] * e, axis=1)
    return mxq(pool, 1, "e4m3") @ mxq(f64(wp), 0, "e4m3")


def e4m3fn_bytes(y):
    return np.clip(np.asarray(y, np.float64), -448.0, 448.0).astype(np.float32).astype(ml_dtypes.float8_e4m3fn).view(np.uint8)


def e4m3fn_values(b):
    return np.asarray(b, np.uint8).view(ml_dtypes.float8_e4m3fn).astype(np.float64)


def setup_inputs():
    d = draw0()
    x0 = np.asarray(d['wp']).astype(np.float64)
    s = (np.max(np.abs(x0), axis=(1,), keepdims=True) / 448.0).astype(np.float32)
    out = {}
    for k, v in d.items():
        if k == 'wp':
            out['wp_bytes'] = e4m3fn_bytes(x0 / s.astype(np.float64))
            out['wp_scale'] = s
        else:
            out[k] = v
    return out


def reference(v, ga, wa, ba, h, gp, wp_bytes, wp_scale):
    return core(v, ga, wa, ba, h, gp, e4m3fn_values(wp_bytes) * wp_scale.astype(np.float64))

@@ -1,0 +1,419 @@
+from contextlib import ExitStack
+
+import concourse.mybir as mybir
+from concourse.masks import make_identity
+
+B, F, D, A, O = 512, 8, 512, 512, 1024
+FLOPS = 2 * B * 28 * D * A + 2 * B * D * O
+
+F32 = mybir.dt.float32
+BF16 = mybir.dt.bfloat16
+U32 = mybir.dt.uint32
+U8 = mybir.dt.uint8
+E4M3 = mybir.dt.float8_e4m3fn
+FP8X4 = mybir.dt.float8_e4m3fn_x4
+MULT = mybir.AluOpType.mult
+ADD = mybir.AluOpType.add
+SUB = mybir.AluOpType.subtract
+MIN = mybir.AluOpType.min
+ACT = mybir.ActivationFunctionType
+AX = mybir.AxisListType
+
+P = 128
+NBT = B // P
+FI = F - 1
+CHUNKS = [
+    [(0, 1, 4)],
+    [(1, 2, 4)],
+    [(2, 3, 4)],
+    [(3, 4, 4)],
+    [(0, 5, 3), (2, 7, 1)],
+    [(4, 5, 3), (6, 7, 1)],
+    [(1, 6, 2), (5, 6, 2)],
+]
+NCH = len(CHUNKS)
+NSLOT = NBT * NCH
+MASKED = float(2.0 ** 100)
+
+
+def tile_afmpairattentionpooling_kernel(tc, v, ga, wa, ba, h, gp, wp_bytes, wp_scale, out):
+    nc = tc.nc
+    with ExitStack() as ctx:
+        keep = ctx.enter_context(tc.tile_pool(name="keep", bufs=1))
+        work = ctx.enter_context(tc.tile_pool(name="work", bufs=2))
+        psum = ctx.enter_context(tc.psum_pool(name="psum", bufs=1))
+        ctx.enter_context(nc.allow_non_contiguous_dma(reason="vectors of 512 onto the partitions"))
+        ctx.enter_context(tc.manual_schedule())
+
+        vn = {}
+        vd = {}
+        vT = {}
+        vg = {}
+        eg = {}
+        codes = {}
+        planes = {}
+        zt = {}
+        st = {}
+        hl = {}
+        pe = {}
+        xb = {}
+        am = {}
+        qt = {}
+        pool_b = {}
+        pool_c = {}
+        pool_s = {}
+        wt = {}
+        al = {}
+        tn_t = {}
+        mn_t = {}
+        den_t = {}
+
+        id32 = keep.tile([P, P], F32, name="id32")
+        idb = keep.tile([P, P], BF16, name="idb")
+        make_identity(nc, id32[:])
+        make_identity(nc, idb[:])
+        zeros = keep.tile([P, 64], BF16, name="zeros")
+        nc.gpsimd.memset(zeros[:], 0.0)
+        invalid = keep.tile([P, FI, F], F32, name="invalid")
+        nc.gpsimd.memset(invalid[:], 0.0)
+        for i in range(FI):
+            nc.gpsimd.memset(invalid[:, i, 0 : i + 1], MASKED)
+
+        def load_v(b, pieces):
+            vn[b] = work.tile([P, F, D], BF16, name="vn", tag="vn", bufs=2)
+            for f0, f1 in pieces:
+                nc.sync.dma_start(out=vn[b][:, f0:f1, :], in_=v[b * P : (b + 1) * P, f0:f1, :])
+
+        def load_vd(b):
+            vd[b] = work.tile([P, 16, D], BF16, name="vd", tag="vd", bufs=2)
+            src = v[b * P : (b + 1) * P].rearrange("(g r) j k -> (r j) g k", r=8)
+            for hh in range(2):
+                nc.sync.dma_start(out=vd[b][64 * hh : 64 * hh + 64], in_=src)
+
+        load_v(0, [(0, 2), (2, 4)])
+        wa_raw = keep.tile([P, 4, A], BF16, name="wa_raw")
+        nc.sync.dma_start(out=wa_raw[:], in_=wa.rearrange("(p j) a -> p j a", j=4))
+        for f0 in (4, 6):
+            nc.sync.dma_start(out=vn[0][:, f0 : f0 + 2, :], in_=v[0:P, f0 : f0 + 2, :])
+        ga_b = keep.tile([P, 4], BF16, name="ga_b")
+        nc.sync.dma_start(out=ga_b[:], in_=ga.rearrange("(p t) -> p t", t=4))
+        ba_b = keep.tile([P, 4, 2], BF16, name="ba_b")
+        nc.sync.dma_start(out=ba_b[:, :, 0], in_=ba.rearrange("(c p) -> p c", p=P))
+        h_b = keep.tile([P, 4, 2], BF16, name="h_b")
+        nc.sync.dma_start(out=h_b[:, :, 0], in_=h.rearrange("(c p) -> p c", p=P))
+        gp_b = keep.tile([P, 4], BF16, name="gp_b")
+        nc.sync.dma_start(out=gp_b[:], in_=gp.rearrange("(p t) -> p t", t=4))
+        wps = keep.tile([P, 4], F32, name="wps")
+        nc.sync.dma_start(out=wps[:], in_=wp_scale.rearrange("(p t) o -> p (t o)", t=4))
+        load_v(1, [(0, 8)])
+        wpb = keep.tile([P, 4, O], U8, name="wpb")
+        nc.sync.dma_start(out=wpb[:], in_=wp_bytes.rearrange("(p t) o -> p t o", t=4))
+        load_vd(0)
+        load_vd(1)
+
+        def turn(b, m):
+            if m == 0:
+                vT[b] = work.tile([P, F, P, 4], BF16, name="vT", tag="vT", bufs=3, align_bytes=64)
+            tp = psum.tile([P, 2, 2, P], F32, name="tp", tag="tp", bufs=1)
+            words = vn[b][:].bitcast(F32)
+            for f in range(2):
+                for u in range(2):
+                    src = words[:, 2 * m + f, :].rearrange("r (w u) -> r u w", u=2)[:, u, :]
+                    nc.tensor.transpose(tp[:, f, u, :], src, id32[:])
+            return tp
+
+        def turn_out(b, m, tp, eng):
+            dst = vT[b][:, 2 * m : 2 * m + 2].bitcast(F32)
+            src = tp[:].rearrange("p f u b -> p f b u")
+            if eng == 0:
+                nc.scalar.copy(out=dst, in_=src)
+            else:
+                nc.vector.tensor_copy(out=dst, in_=src)
+
+        def gains(b, i0, i1):
+            if b not in vg:
+                vg[b] = work.tile([P, 4, FI, P], F32, name="vg", tag="vg", bufs=2, align_bytes=64)
+            for t in range(4):
+                nc.scalar.activation(
+                    out=vg[b][:, t, i0:i1, :], in_=vT[b][:, i0:i1, :, t], func=ACT.Copy, scale=ga_f[:, t : t + 1]
+                )
+
+        def products(s):
+            b, c = divmod(s, NCH)
+            eg[s] = work.tile([P, 4, P, 4], BF16, name="eg", tag="eg", bufs=3, align_bytes=64)
+            o = 0
+            for i, j0, n in CHUNKS[c]:
+                left = vg[b][:, :, i, :].rearrange("p t b -> p b t").unsqueeze(1).to_broadcast([P, n, P, 4])
+                nc.vector.tensor_tensor(out=eg[s][:, o : o + n], in0=left, in1=vT[b][:, j0 : j0 + n], op=MULT)
+                o += n
+
+        def quantize(s):
+            codes[s] = work.tile([P, 512], U32, name="codes", tag="codes", bufs=3, align_bytes=64)
+            planes[s] = work.tile([P, 512], U8, name="planes", tag="planes", bufs=3, align_bytes=64)
+            nc.vector.quantize_mx(
+                out=codes[s][:].bitcast(FP8X4), scales=planes[s][:], in_=eg[s][:].rearrange("p q b t -> p (q b t)")
+            )
+
+        def hidden(s):
+            zt[s] = work.tile([P, 4, 512], F32, name="zt", tag="zt", bufs=3)
+            for c in range(4):
+                mx = psum.tile([P, 512], F32, name="mx", tag="mx", bufs=4)
+                nc.tensor.matmul_mx(
+                    out=mx[:],
+                    lhsT=wa_codes[:, c * P : (c + 1) * P].bitcast(FP8X4),
+                    lhsT_scale=wa_planes[:, c * P : (c + 1) * P],
+                    rhs=codes[s][:].bitcast(FP8X4),
+                    rhs_scale=planes[s][:],
+                    start=True,
+                    stop=True,
+                )
+                nc.scalar.activation(out=zt[s][:, c, :], in_=mx[:], func=ACT.Relu, bias=ba_f[:, c : c + 1], scale=1.0)
+
+        def scores(s):
+            b, c = divmod(s, NCH)
+            if c == 0:
+                st[b] = psum.tile([P, FI * F], F32, name="st", tag="st", bufs=1)
+                nc.tensor.matmul(out=st[b][:], lhsT=idb[:], rhs=zeros[:, 0 : FI * F], start=True, stop=True)
+            q = 0
+            for i, j0, n in CHUNKS[c]:
+                for j in range(j0, j0 + n):
+                    col = i * F + j
+                    for a in range(4):
+                        nc.tensor.matmul(
+                            out=st[b][:, col : col + 1],
+                            lhsT=zt[s][:, a, q * P : (q + 1) * P],
+                            rhs=h_f[:, a : a + 1],
+                            start=(a == 0),
+                            stop=(a == 3),
+                        )
+                    q += 1
+
+        def soft_a(b):
+            tn_t[b] = work.tile([P, FI * F], F32, name="tn", tag="tn")
+            nc.vector.scalar_tensor_tensor(
+                out=tn_t[b][:], in0=st[b][:], scalar=-1.0, in1=invalid[:].rearrange("p i j -> p (i j)"), op0=MULT, op1=ADD
+            )
+
+        def soft_b(b):
+            mn_t[b] = work.tile([P, 1], F32, name="mn", tag="mn")
+            nc.vector.tensor_reduce(out=mn_t[b][:], in_=tn_t[b][:], axis=AX.X, op=MIN)
+
+        def soft_c(b):
+            pe[b] = work.tile([P, FI, F], F32, name="pe", tag="pe")
+            den_t[b] = work.tile([P, 1], F32, name="den", tag="den")
+            nc.scalar.activation(
+                out=pe[b][:].rearrange("p i j -> p (i j)"), in_=tn_t[b][:], func=ACT.Exp, bias=mn_t[b][:], scale=-1.0,
+                accum_out=den_t[b][:],
+            )
+
+        def soft_d(b):
+            inv = work.tile([P, 1], F32, name="inv", tag="inv")
+            nc.vector.reciprocal(out=inv[:], in_=den_t[b][:])
+            hl[b] = work.tile([P, FI, 2, F], BF16, name="hl", tag="hl")
+            al[b] = work.tile([P, FI, F], F32, name="al", tag="al")
+            nc.vector.tensor_scalar(out=al[b][:], in0=pe[b][:], scalar1=inv[:], scalar2=None, op0=MULT)
+            nc.vector.tensor_copy(out=hl[b][:, :, 0, :], in_=al[b][:])
+            nc.vector.tensor_tensor(out=hl[b][:, :, 1, :], in0=al[b][:], in1=hl[b][:, :, 0, :], op=SUB)
+
+        def spread_a(b):
+            xb[b] = work.tile([P, FI * 2, 8, F], BF16, name="xb", tag="xb")
+            src = hl[b][:].rearrange("p i h j -> p (i h) j").unsqueeze(2).to_broadcast([P, FI * 2, 8, F])
+            nc.scalar.copy(out=xb[b][:], in_=src)
+
+        def spread_b(b):
+            tp = psum.tile([P, FI, P], BF16, name="tpb", tag="tp", bufs=1)
+            flat = xb[b][:].rearrange("p x r j -> p (x r j)")
+            for i in range(FI):
+                nc.tensor.transpose(tp[:, i, :], flat[:, i * P : (i + 1) * P], idb[:])
+            return tp
+
+        def spread_c(b, tp):
+            am[b] = work.tile([P, 16, FI, 8], BF16, name="am", tag="am")
+            nc.vector.tensor_tensor(
+                out=am[b][:].rearrange("m g i r -> m i g r"),
+                in0=tp[:].rearrange("m i (g r) -> m i g r", r=8),
+                in1=mask[:].unsqueeze(1).unsqueeze(1).to_broadcast([P, FI, 16, 8]),
+                op=MULT,
+            )
+
+        def weigh(b, hh, t):
+            wt[b, hh, t] = psum.tile([P, FI, 64], F32, name="wt", tag="wt", bufs=2)
+            for g in range(8):
+                nc.tensor.matmul(
+                    out=wt[b, hh, t][:, :, 8 * g : 8 * g + 8],
+                    lhsT=vd[b][:, 8 * hh + g, :].rearrange("m (p t) -> m t p", t=4)[:, t, :],
+                    rhs=am[b][:, 8 * hh + g],
+                    start=True,
+                    stop=True,
+                )
+
+        def weigh_out(b, hh, t):
+            if t == 0:
+                qt[b, hh] = work.tile([P, 4, FI, 64], F32, name="qt", tag="qt", bufs=2)
+            nc.vector.scalar_tensor_tensor(
+                out=qt[b, hh][:, t], in0=wt[b, hh, t][:], scalar=gp_f[:, t : t + 1],
+                in1=vT[b][:, 0:FI, 64 * hh : 64 * hh + 64, t], op0=MULT, op1=MULT,
+            )
+
+        def add_up(b, hh):
+            if hh == 0:
+                pool_b[b] = work.tile([P, P, 4], BF16, name="pool_b", tag="pool_b", align_bytes=64)
+            q = qt[b, hh]
+            r = work.tile([P, 4, 3, 64], F32, name="radd", tag="radd", bufs=1)
+            r0 = work.tile([P, 4, 64], F32, name="radd0", tag="radd0", bufs=1)
+            r1 = work.tile([P, 4, 64], F32, name="radd1", tag="radd1", bufs=1)
+            nc.vector.tensor_tensor(out=r[:], in0=q[:, :, 0:3, :], in1=q[:, :, 3:6, :], op=ADD)
+            nc.vector.tensor_tensor(out=r0[:], in0=r[:, :, 0, :], in1=r[:, :, 1, :], op=ADD)
+            nc.vector.tensor_tensor(out=r1[:], in0=r[:, :, 2, :], in1=q[:, :, 6, :], op=ADD)
+            nc.vector.tensor_tensor(
+                out=pool_b[b][:, 64 * hh : 64 * hh + 64, :],
+                in0=r0[:].rearrange("p t b -> p b t"),
+                in1=r1[:].rearrange("p t b -> p b t"),
+                op=ADD,
+            )
+
+        def pool_quant(b):
+            pool_c[b] = work.tile([P, P], U32, name="pool_c", tag="pool_c", align_bytes=64)
+            pool_s[b] = work.tile([P, P], U8, name="pool_s", tag="pool_s", align_bytes=64)
+            nc.vector.quantize_mx(
+                out=pool_c[b][:].bitcast(FP8X4), scales=pool_s[b][:], in_=pool_b[b][:].rearrange("p b t -> p (b t)")
+            )
+
+        def head_out(b):
+            osb = work.tile([P, O], F32, name="osb", tag="osb", bufs=2)
+            for n in range(2):
+                cols = slice(512 * n, 512 * n + 512)
+                mx = psum.tile([P, 512], F32, name="mx", tag="mx", bufs=4)
+                nc.tensor.matmul_mx(
+                    out=mx[:],
+                    lhsT=pool_c[b][:].bitcast(FP8X4),
+                    lhsT_scale=pool_s[b][:],
+                    rhs=wp_codes[:, cols].bitcast(FP8X4),
+                    rhs_scale=wp_planes[:, cols],
+                    start=True,
+                    stop=True,
+                )
+                nc.scalar.copy(out=osb[:, cols], in_=mx[:])
+                nc.sync.dma_start(out=out[b * P : (b + 1) * P, cols], in_=osb[:, cols])
+
+        tps = []
+        for m in range(4):
+            tp = turn(0, m)
+            turn_out(0, m, tp, m % 2)
+            if m == 0:
+                ga_f = keep.tile([P, 4], F32, name="ga_f")
+                nc.vector.tensor_copy(out=ga_f[:], in_=ga_b[:])
+                gains(0, 0, 2)
+            if m == 1:
+                wa_g = keep.tile([P, A, 4], BF16, name="wa_g", align_bytes=64)
+                nc.vector.tensor_copy(out=wa_g[:], in_=wa_raw[:].rearrange("p j a -> p a j"))
+        gains(0, 2, 7)
+        mask = keep.tile([P, 8], BF16, name="mask")
+        with nc.allow_low_precision(reason="sums of zeros and a single one"):
+            nc.vector.tensor_reduce(
+                out=mask[:], in_=idb[:].rearrange("p (h r j) -> p r h j", h=2, r=8), axis=AX.XY, op=ADD
+            )
+        products(0)
+        wa_codes = keep.tile([P, A], U32, name="wa_codes", align_bytes=64)
+        wa_planes = keep.tile([P, A], U8, name="wa_planes", align_bytes=64)
+        nc.vector.quantize_mx(
+            out=wa_codes[:].bitcast(FP8X4), scales=wa_planes[:], in_=wa_g[:].rearrange("p a j -> p (a j)")
+        )
+        quantize(0)
+        ba_f = keep.tile([P, 4], F32, name="ba_f")
+        nc.vector.tensor_copy(out=ba_f[:], in_=ba_b[:, :, 0])
+        h_f = keep.tile([P, 4], F32, name="h_f")
+        nc.vector.tensor_copy(out=h_f[:], in_=h_b[:, :, 0])
+        gp_f = keep.tile([P, 4], F32, name="gp_f")
+        nc.vector.tensor_copy(out=gp_f[:], in_=gp_b[:])
+        products(1)
+
+        wpl = keep.tile([P, 4, O], BF16, name="wpl")
+        wpg = keep.tile([P, O, 4], BF16, name="wpg", align_bytes=64)
+        wp_codes = keep.tile([P, O], U32, name="wp_codes", align_bytes=64)
+        wp_planes = keep.tile([P, O], U8, name="wp_planes", align_bytes=64)
+
+        tail = 10
+        tpb = {}
+        for s in range(NSLOT + tail):
+            b, c = divmod(s, NCH)
+            live = s < NSLOT
+            if c == 2 and b >= 1 and b - 1 < NBT:
+                spread_a(b - 1)
+            if live:
+                hidden(s)
+            pb = b - 1
+            if 0 <= pb < NBT and 3 <= c <= 6:
+                hh, t0 = divmod(2 * (c - 3), 4)
+                weigh(pb, hh, t0)
+                weigh(pb, hh, t0 + 1)
+            todo = []
+            if live and b + 1 < NBT:
+                if c == 1:
+                    todo.append((1, turn(b + 1, 1)))
+                if c == 2:
+                    todo.append((3, turn(b + 1, 3)))
+                for m, tp in todo:
+                    turn_out(b + 1, m, tp, 0)
+            if c == 1 and 0 <= pb < NBT:
+                soft_a(pb)
+            if 1 <= s <= NSLOT:
+                scores(s - 1)
+            if s + 2 < NSLOT:
+                products(s + 2)
+            if c == 1 and 0 <= pb < NBT:
+                soft_b(pb)
+                soft_c(pb)
+            if 0 <= pb < NBT and 3 <= c <= 6:
+                weigh_out(pb, hh, t0)
+            if s + 1 < NSLOT:
+                quantize(s + 1)
+            if 0 <= pb < NBT and 3 <= c <= 6:
+                weigh_out(pb, hh, t0 + 1)
+            if c == 1 and 0 <= pb < NBT:
+                soft_d(pb)
+            if live and b + 1 < NBT:
+                if c == 0:
+                    tp = turn(b + 1, 0)
+                    turn_out(b + 1, 0, tp, 0)
+                if c == 1:
+                    tp = turn(b + 1, 2)
+                    turn_out(b + 1, 2, tp, 0)
+                if c == 3:
+                    gains(b + 1, 0, 2)
+                if c == 4:
+                    gains(b + 1, 2, 4)
+                if c == 5:
+                    gains(b + 1, 4, 7)
+            if c == 2 and 0 <= pb < NBT:
+                tp = spread_b(pb)
+                spread_c(pb, tp)
+            if c == 5 and 0 <= pb < NBT:
+                add_up(pb, 0)
+            if c == 0 and 0 <= b - 2 < NBT:
+                add_up(b - 2, 1)
+            if c == 1 and 0 <= b - 2 < NBT:
+                pool_quant(b - 2)
+            if c == 2 and 0 <= b - 2 < NBT:
+                head_out(b - 2)
+            if s == 0:
+                load_v(2, [(0, 8)])
+            if s == 3:
+                load_v(3, [(0, 8)])
+            if s == 14:
+                load_vd(2)
+            if s == 21:
+                load_vd(3)
+            if s < 4:
+                nc.scalar.activation(
+                    out=wpl[:, s, :], in_=wpb[:, s, :].bitcast(E4M3), func=ACT.Copy, scale=wps[:, s : s + 1]
+                )
+            if 7 <= s < 11:
+                n0 = 256 * (s - 7)
+                nc.scalar.copy(
+                    out=wpg[:, n0 : n0 + 256, :], in_=wpl[:, :, n0 : n0 + 256].rearrange("p j n -> p n j")
+                )
+            if s == 12:
+                nc.vector.quantize_mx(
+                    out=wp_codes[:].bitcast(FP8X4), scales=wp_planes[:], in_=wpg[:].rearrange("p n j -> p (n j)")
+                )

@@ -15,6 +15,7 @@ FP8X4 = mybir.dt.float8_e4m3fn_x4
 MULT = mybir.AluOpType.mult
 ADD = mybir.AluOpType.add
 SUB = mybir.AluOpType.subtract
+MAX = mybir.AluOpType.max
 MIN = mybir.AluOpType.min
 ACT = mybir.ActivationFunctionType
 AX = mybir.AxisListType
@@ -31,9 +32,22 @@ CHUNKS = [
     [(4, 5, 3), (6, 7, 1)],
     [(1, 6, 2), (5, 6, 2)],
 ]
+CHUNKS_FIRST = [
+    [(0, 1, 3), (1, 2, 1)],
+    [(1, 3, 2), (2, 3, 2)],
+    [(0, 4, 4)],
+    [(1, 5, 3), (2, 5, 1)],
+    [(2, 6, 2), (3, 4, 2)],
+    [(3, 6, 2), (4, 5, 2)],
+    [(4, 7, 1), (5, 6, 2), (6, 7, 1)],
+]
 NCH = len(CHUNKS)
 NSLOT = NBT * NCH
 MASKED = float(2.0 ** 100)
+
+
+def chunk(b, c):
+    return CHUNKS_FIRST[c] if b == 0 else CHUNKS[c]
 
 
 def tile_afmpairattentionpooling_kernel(tc, v, ga, wa, ba, h, gp, wp_bytes, wp_scale, out):
@@ -53,18 +67,20 @@ def tile_afmpairattentionpooling_kernel(tc, v, ga, wa, ba, h, gp, wp_bytes, wp_s
         codes = {}
         planes = {}
         zt = {}
-        st = {}
+        mxs = {}
+        ut = {}
         hl = {}
         pe = {}
         xb = {}
         am = {}
         qt = {}
         pool_b = {}
+        pool_n = {}
+        pn = {}
         pool_c = {}
         pool_s = {}
         wt = {}
         al = {}
-        tn_t = {}
         mn_t = {}
         den_t = {}
 
@@ -72,12 +88,13 @@ def tile_afmpairattentionpooling_kernel(tc, v, ga, wa, ba, h, gp, wp_bytes, wp_s
         idb = keep.tile([P, P], BF16, name="idb")
         make_identity(nc, id32[:])
         make_identity(nc, idb[:])
-        zeros = keep.tile([P, 64], BF16, name="zeros")
-        nc.gpsimd.memset(zeros[:], 0.0)
-        invalid = keep.tile([P, FI, F], F32, name="invalid")
-        nc.gpsimd.memset(invalid[:], 0.0)
-        for i in range(FI):
-            nc.gpsimd.memset(invalid[:, i, 0 : i + 1], MASKED)
+        neg = []
+        for n in range(2):
+            t = keep.tile([P, FI, F], F32, name="neg%d" % n)
+            for i in range(FI):
+                nc.gpsimd.memset(t[:, i, 0 : i + 1], MASKED)
+            neg.append(t)
+        junk = keep.tile([P, P], BF16, name="junk")
 
         def load_v(b, pieces):
             vn[b] = work.tile([P, F, D], BF16, name="vn", tag="vn", bufs=2)
@@ -90,19 +107,20 @@ def tile_afmpairattentionpooling_kernel(tc, v, ga, wa, ba, h, gp, wp_bytes, wp_s
             for hh in range(2):
                 nc.sync.dma_start(out=vd[b][64 * hh : 64 * hh + 64], in_=src)
 
-        load_v(0, [(0, 2), (2, 4)])
+        load_v(0, [(0, 2)])
+        ga_b = keep.tile([P, 4], BF16, name="ga_b")
+        nc.sync.dma_start(out=ga_b[:], in_=ga.rearrange("(p t) -> p t", t=4))
+        nc.sync.dma_start(out=vn[0][:, 2:4, :], in_=v[0:P, 2:4, :])
         wa_raw = keep.tile([P, 4, A], BF16, name="wa_raw")
         nc.sync.dma_start(out=wa_raw[:], in_=wa.rearrange("(p j) a -> p j a", j=4))
         for f0 in (4, 6):
             nc.sync.dma_start(out=vn[0][:, f0 : f0 + 2, :], in_=v[0:P, f0 : f0 + 2, :])
-        ga_b = keep.tile([P, 4], BF16, name="ga_b")
-        nc.sync.dma_start(out=ga_b[:], in_=ga.rearrange("(p t) -> p t", t=4))
         ba_b = keep.tile([P, 4, 2], BF16, name="ba_b")
         nc.sync.dma_start(out=ba_b[:, :, 0], in_=ba.rearrange("(c p) -> p c", p=P))
         h_b = keep.tile([P, 4, 2], BF16, name="h_b")
         nc.sync.dma_start(out=h_b[:, :, 0], in_=h.rearrange("(c p) -> p c", p=P))
-        gp_b = keep.tile([P, 4], BF16, name="gp_b")
-        nc.sync.dma_start(out=gp_b[:], in_=gp.rearrange("(p t) -> p t", t=4))
+        gp_r = keep.tile([P, D], BF16, name="gp_r")
+        nc.sync.dma_start(out=gp_r[:], in_=gp.partition_broadcast(P))
         wps = keep.tile([P, 4], F32, name="wps")
         nc.sync.dma_start(out=wps[:], in_=wp_scale.rearrange("(p t) o -> p (t o)", t=4))
         load_v(1, [(0, 8)])
@@ -114,7 +132,10 @@ def tile_afmpairattentionpooling_kernel(tc, v, ga, wa, ba, h, gp, wp_bytes, wp_s
         def turn(b, m):
             if m == 0:
                 vT[b] = work.tile([P, F, P, 4], BF16, name="vT", tag="vT", bufs=3, align_bytes=64)
-            tp = psum.tile([P, 2, 2, P], F32, name="tp", tag="tp", bufs=1)
+            if b == 0:
+                tp = psum.tile([P, 2, 2, P], F32, name="tp", tag="mx", bufs=4)
+            else:
+                tp = psum.tile([P, 2, 2, P], F32, name="tp", tag="tp", bufs=1)
             words = vn[b][:].bitcast(F32)
             for f in range(2):
                 for u in range(2):
@@ -142,7 +163,7 @@ def tile_afmpairattentionpooling_kernel(tc, v, ga, wa, ba, h, gp, wp_bytes, wp_s
             b, c = divmod(s, NCH)
             eg[s] = work.tile([P, 4, P, 4], BF16, name="eg", tag="eg", bufs=3, align_bytes=64)
             o = 0
-            for i, j0, n in CHUNKS[c]:
+            for i, j0, n in chunk(b, c):
                 left = vg[b][:, :, i, :].rearrange("p t b -> p b t").unsqueeze(1).to_broadcast([P, n, P, 4])
                 nc.vector.tensor_tensor(out=eg[s][:, o : o + n], in0=left, in1=vT[b][:, j0 : j0 + n], op=MULT)
                 o += n
@@ -156,53 +177,74 @@ def tile_afmpairattentionpooling_kernel(tc, v, ga, wa, ba, h, gp, wp_bytes, wp_s
 
         def hidden(s):
             zt[s] = work.tile([P, 4, 512], F32, name="zt", tag="zt", bufs=3)
-            for c in range(4):
+            for a in range(4):
                 mx = psum.tile([P, 512], F32, name="mx", tag="mx", bufs=4)
+                mxs[s, a] = mx
                 nc.tensor.matmul_mx(
                     out=mx[:],
-                    lhsT=wa_codes[:, c * P : (c + 1) * P].bitcast(FP8X4),
-                    lhsT_scale=wa_planes[:, c * P : (c + 1) * P],
+                    lhsT=wa_codes[:, a * P : (a + 1) * P].bitcast(FP8X4),
+                    lhsT_scale=wa_planes[:, a * P : (a + 1) * P],
                     rhs=codes[s][:].bitcast(FP8X4),
                     rhs_scale=planes[s][:],
                     start=True,
                     stop=True,
                 )
-                nc.scalar.activation(out=zt[s][:, c, :], in_=mx[:], func=ACT.Relu, bias=ba_f[:, c : c + 1], scale=1.0)
+
+        def on_vector(s, a):
+            return a == 3 or (a == 2 and s % 3 != 2)
+
+        def weigh_s(s):
+            mine = [a for a in range(4) if not on_vector(s, a)]
+            for a in mine:
+                nc.scalar.activation(
+                    out=zt[s][:, a, :], in_=mxs[s, a][:], func=ACT.Relu, bias=ba_f[:, a : a + 1], scale=1.0
+                )
+            for a in mine:
+                nc.scalar.activation(
+                    out=zt[s][:, a, :], in_=zt[s][:, a, :], func=ACT.Identity, bias=nhba[:, a : a + 1],
+                    scale=h_f[:, a : a + 1],
+                )
+
+        def weigh_v(s):
+            for a in range(4):
+                if on_vector(s, a):
+                    nc.vector.tensor_scalar(
+                        out=zt[s][:, a, :], in0=mxs[s, a][:], scalar1=nba[:, a : a + 1], scalar2=h_f[:, a : a + 1],
+                        op0=MAX, op1=MULT,
+                    )
 
         def scores(s):
-            b, c = divmod(s, NCH)
-            if c == 0:
-                st[b] = psum.tile([P, FI * F], F32, name="st", tag="st", bufs=1)
-                nc.tensor.matmul(out=st[b][:], lhsT=idb[:], rhs=zeros[:, 0 : FI * F], start=True, stop=True)
-            q = 0
-            for i, j0, n in CHUNKS[c]:
-                for j in range(j0, j0 + n):
-                    col = i * F + j
-                    for a in range(4):
-                        nc.tensor.matmul(
-                            out=st[b][:, col : col + 1],
-                            lhsT=zt[s][:, a, q * P : (q + 1) * P],
-                            rhs=h_f[:, a : a + 1],
-                            start=(a == 0),
-                            stop=(a == 3),
-                        )
-                    q += 1
+            ut[s] = psum.tile([P, 4, P], F32, name="ut", tag="ut", bufs=1)
+            for q in range(4):
+                for a in range(4):
+                    nc.tensor.matmul(
+                        out=ut[s][:, q, :],
+                        lhsT=zt[s][:, a, q * P : (q + 1) * P],
+                        rhs=id32[:],
+                        start=(a == 0),
+                        stop=(a == 3),
+                        is_transpose=True,
+                    )
 
-        def soft_a(b):
-            tn_t[b] = work.tile([P, FI * F], F32, name="tn", tag="tn")
-            nc.vector.scalar_tensor_tensor(
-                out=tn_t[b][:], in0=st[b][:], scalar=-1.0, in1=invalid[:].rearrange("p i j -> p (i j)"), op0=MULT, op1=ADD
-            )
+        def sums(s):
+            b, c = divmod(s, NCH)
+            q = 0
+            for i, j0, n in chunk(b, c):
+                for j in range(j0, j0 + n):
+                    nc.scalar.activation(
+                        out=junk[:], in_=ut[s][:, q, :], func=ACT.Copy, scale=-1.0, accum_out=neg[b % 2][:, i, j : j + 1]
+                    )
+                    q += 1
 
         def soft_b(b):
             mn_t[b] = work.tile([P, 1], F32, name="mn", tag="mn")
-            nc.vector.tensor_reduce(out=mn_t[b][:], in_=tn_t[b][:], axis=AX.X, op=MIN)
+            nc.vector.tensor_reduce(out=mn_t[b][:], in_=neg[b % 2][:].rearrange("p i j -> p (i j)"), axis=AX.X, op=MIN)
 
         def soft_c(b):
             pe[b] = work.tile([P, FI, F], F32, name="pe", tag="pe")
             den_t[b] = work.tile([P, 1], F32, name="den", tag="den")
             nc.scalar.activation(
-                out=pe[b][:].rearrange("p i j -> p (i j)"), in_=tn_t[b][:], func=ACT.Exp, bias=mn_t[b][:], scale=-1.0,
+                out=pe[b][:].rearrange("p i j -> p (i j)"), in_=neg[b % 2][:].rearrange("p i j -> p (i j)"), func=ACT.Exp, bias=mn_t[b][:], scale=-1.0,
                 accum_out=den_t[b][:],
             )
 
@@ -237,7 +279,10 @@ def tile_afmpairattentionpooling_kernel(tc, v, ga, wa, ba, h, gp, wp_bytes, wp_s
             )
 
         def weigh(b, hh, t):
-            wt[b, hh, t] = psum.tile([P, FI, 64], F32, name="wt", tag="wt", bufs=2)
+            if b == NBT - 1:
+                wt[b, hh, t] = psum.tile([P, FI, 64], F32, name="wt", tag="mx", bufs=4)
+            else:
+                wt[b, hh, t] = psum.tile([P, FI, 64], F32, name="wt", tag="wt", bufs=1)
             for g in range(8):
                 nc.tensor.matmul(
                     out=wt[b, hh, t][:, :, 8 * g : 8 * g + 8],
@@ -248,29 +293,38 @@ def tile_afmpairattentionpooling_kernel(tc, v, ga, wa, ba, h, gp, wp_bytes, wp_s
                 )
 
         def weigh_out(b, hh, t):
-            if t == 0:
-                qt[b, hh] = work.tile([P, 4, FI, 64], F32, name="qt", tag="qt", bufs=2)
-            nc.vector.scalar_tensor_tensor(
-                out=qt[b, hh][:, t], in0=wt[b, hh, t][:], scalar=gp_f[:, t : t + 1],
-                in1=vT[b][:, 0:FI, 64 * hh : 64 * hh + 64, t], op0=MULT, op1=MULT,
+            if b not in qt:
+                qt[b] = work.tile([P, 4, FI, P], F32, name="qt", tag="qt", bufs=1)
+            cols = slice(64 * hh, 64 * hh + 64)
+            nc.vector.tensor_tensor(
+                out=qt[b][:, t, :, cols], in0=wt[b, hh, t][:], in1=vT[b][:, 0:FI, cols, t], op=MULT
             )
 
-        def add_up(b, hh):
-            if hh == 0:
-                pool_b[b] = work.tile([P, P, 4], BF16, name="pool_b", tag="pool_b", align_bytes=64)
-            q = qt[b, hh]
-            r = work.tile([P, 4, 3, 64], F32, name="radd", tag="radd", bufs=1)
-            r0 = work.tile([P, 4, 64], F32, name="radd0", tag="radd0", bufs=1)
-            r1 = work.tile([P, 4, 64], F32, name="radd1", tag="radd1", bufs=1)
-            nc.vector.tensor_tensor(out=r[:], in0=q[:, :, 0:3, :], in1=q[:, :, 3:6, :], op=ADD)
-            nc.vector.tensor_tensor(out=r0[:], in0=r[:, :, 0, :], in1=r[:, :, 1, :], op=ADD)
-            nc.vector.tensor_tensor(out=r1[:], in0=r[:, :, 2, :], in1=q[:, :, 6, :], op=ADD)
+        def add_up(b, t):
+            if t == 0:
+                pn[b] = psum.tile([P, 4, P], F32, name="pn", tag="pn", bufs=1)
+            for i in range(FI):
+                nc.tensor.matmul(
+                    out=pn[b][:, t, :], lhsT=qt[b][:, t, i, :], rhs=id32[:], start=(i == 0), stop=(i == FI - 1),
+                    is_transpose=True,
+                )
+
+        def pool_gain(b):
+            pool_n[b] = work.tile([P, P, 4], BF16, name="pool_n", tag="pool_n")
             nc.vector.tensor_tensor(
-                out=pool_b[b][:, 64 * hh : 64 * hh + 64, :],
-                in0=r0[:].rearrange("p t b -> p b t"),
-                in1=r1[:].rearrange("p t b -> p b t"),
-                op=ADD,
+                out=pool_n[b][:],
+                in0=pn[b][:].rearrange("b t p -> b p t"),
+                in1=gp_r[:].rearrange("b (p t) -> b p t", t=4),
+                op=MULT,
             )
+
+        def pool_turn(b):
+            tp = psum.tile([P, 2, P], F32, name="tpp", tag="tp", bufs=1)
+            words = pool_n[b][:].rearrange("b p t -> b (p t)").bitcast(F32).rearrange("b (w u) -> b u w", u=2)
+            for u in range(2):
+                nc.tensor.transpose(tp[:, u, :], words[:, u, :], id32[:])
+            pool_b[b] = work.tile([P, P, 4], BF16, name="pool_b", tag="pool_b", align_bytes=64)
+            nc.scalar.copy(out=pool_b[b][:].bitcast(F32), in_=tp[:].rearrange("p u b -> p b u"))
 
         def pool_quant(b):
             pool_c[b] = work.tile([P, P], U32, name="pool_c", tag="pool_c", align_bytes=64)
@@ -296,36 +350,37 @@ def tile_afmpairattentionpooling_kernel(tc, v, ga, wa, ba, h, gp, wp_bytes, wp_s
                 nc.scalar.copy(out=osb[:, cols], in_=mx[:])
                 nc.sync.dma_start(out=out[b * P : (b + 1) * P, cols], in_=osb[:, cols])
 
-        tps = []
+        ga_f = keep.tile([P, 4], F32, name="ga_f")
+        nc.gpsimd.tensor_copy(out=ga_f[:], in_=ga_b[:])
         for m in range(4):
             tp = turn(0, m)
-            turn_out(0, m, tp, m % 2)
+            turn_out(0, m, tp, m == 1)
             if m == 0:
-                ga_f = keep.tile([P, 4], F32, name="ga_f")
-                nc.vector.tensor_copy(out=ga_f[:], in_=ga_b[:])
                 gains(0, 0, 2)
-            if m == 1:
-                wa_g = keep.tile([P, A, 4], BF16, name="wa_g", align_bytes=64)
-                nc.vector.tensor_copy(out=wa_g[:], in_=wa_raw[:].rearrange("p j a -> p a j"))
-        gains(0, 2, 7)
-        mask = keep.tile([P, 8], BF16, name="mask")
-        with nc.allow_low_precision(reason="sums of zeros and a single one"):
-            nc.vector.tensor_reduce(
-                out=mask[:], in_=idb[:].rearrange("p (h r j) -> p r h j", h=2, r=8), axis=AX.XY, op=ADD
-            )
         products(0)
+        gains(0, 2, 7)
+        wa_g = keep.tile([P, A, 4], BF16, name="wa_g", align_bytes=64)
+        nc.vector.tensor_copy(out=wa_g[:], in_=wa_raw[:].rearrange("p j a -> p a j"))
+        quantize(0)
         wa_codes = keep.tile([P, A], U32, name="wa_codes", align_bytes=64)
         wa_planes = keep.tile([P, A], U8, name="wa_planes", align_bytes=64)
         nc.vector.quantize_mx(
             out=wa_codes[:].bitcast(FP8X4), scales=wa_planes[:], in_=wa_g[:].rearrange("p a j -> p (a j)")
         )
-        quantize(0)
+        mask = keep.tile([P, 8], BF16, name="mask")
+        with nc.allow_low_precision(reason="sums of zeros and a single one"):
+            nc.vector.tensor_reduce(
+                out=mask[:], in_=idb[:].rearrange("p (h r j) -> p r h j", h=2, r=8), axis=AX.XY, op=ADD
+            )
         ba_f = keep.tile([P, 4], F32, name="ba_f")
-        nc.vector.tensor_copy(out=ba_f[:], in_=ba_b[:, :, 0])
+        nc.gpsimd.tensor_copy(out=ba_f[:], in_=ba_b[:, :, 0])
         h_f = keep.tile([P, 4], F32, name="h_f")
-        nc.vector.tensor_copy(out=h_f[:], in_=h_b[:, :, 0])
-        gp_f = keep.tile([P, 4], F32, name="gp_f")
-        nc.vector.tensor_copy(out=gp_f[:], in_=gp_b[:])
+        nc.gpsimd.tensor_copy(out=h_f[:], in_=h_b[:, :, 0])
+        nba = keep.tile([P, 4], F32, name="nba")
+        nc.gpsimd.tensor_scalar(out=nba[:], in0=ba_f[:], scalar1=-1.0, scalar2=None, op0=MULT)
+        nhba = keep.tile([P, 4], F32, name="nhba")
+        nc.gpsimd.tensor_tensor(out=nhba[:], in0=h_f[:], in1=nba[:], op=MULT)
+        hidden(0)
         products(1)
 
         wpl = keep.tile([P, 4, O], BF16, name="wpl")
@@ -334,75 +389,76 @@ def tile_afmpairattentionpooling_kernel(tc, v, ga, wa, ba, h, gp, wp_bytes, wp_s
         wp_planes = keep.tile([P, O], U8, name="wp_planes", align_bytes=64)
 
         tail = 10
-        tpb = {}
         for s in range(NSLOT + tail):
             b, c = divmod(s, NCH)
             live = s < NSLOT
-            if c == 2 and b >= 1 and b - 1 < NBT:
-                spread_a(b - 1)
+            turning = live and b + 1 < NBT
+
+            off = {}
+            for bb in range(NBT):
+                k = s - NCH * (bb + 1)
+                if 0 <= k <= 12:
+                    off[k] = bb
+
+            if 2 <= s <= NSLOT + 1:
+                sums(s - 2)
             if live:
-                hidden(s)
-            pb = b - 1
-            if 0 <= pb < NBT and 3 <= c <= 6:
-                hh, t0 = divmod(2 * (c - 3), 4)
-                weigh(pb, hh, t0)
-                weigh(pb, hh, t0 + 1)
-            todo = []
-            if live and b + 1 < NBT:
-                if c == 1:
-                    todo.append((1, turn(b + 1, 1)))
-                if c == 2:
-                    todo.append((3, turn(b + 1, 3)))
-                for m, tp in todo:
-                    turn_out(b + 1, m, tp, 0)
-            if c == 1 and 0 <= pb < NBT:
-                soft_a(pb)
+                weigh_s(s)
+                weigh_v(s)
+            if 1 in off:
+                soft_b(off[1])
+                soft_c(off[1])
+            if 2 in off:
+                tp = spread_b(off[2])
+                spread_c(off[2], tp)
+            for t in range(4):
+                if t + 3 in off:
+                    weigh(off[t + 3], 0, t)
+                    weigh_out(off[t + 3], 0, t)
+                if t + 4 in off:
+                    add_up(off[t + 4], t)
             if 1 <= s <= NSLOT:
                 scores(s - 1)
-            if s + 2 < NSLOT:
-                products(s + 2)
-            if c == 1 and 0 <= pb < NBT:
-                soft_b(pb)
-                soft_c(pb)
-            if 0 <= pb < NBT and 3 <= c <= 6:
-                weigh_out(pb, hh, t0)
             if s + 1 < NSLOT:
                 quantize(s + 1)
-            if 0 <= pb < NBT and 3 <= c <= 6:
-                weigh_out(pb, hh, t0 + 1)
-            if c == 1 and 0 <= pb < NBT:
-                soft_d(pb)
-            if live and b + 1 < NBT:
-                if c == 0:
-                    tp = turn(b + 1, 0)
-                    turn_out(b + 1, 0, tp, 0)
+            if 9 in off:
+                pool_quant(off[9])
+            if 1 in off:
+                soft_d(off[1])
+                spread_a(off[1])
+            if s + 2 < NSLOT:
+                products(s + 2)
+            for t in range(4):
+                if t + 3 in off:
+                    weigh(off[t + 3], 1, t)
+                    weigh_out(off[t + 3], 1, t)
+            if s + 1 < NSLOT:
+                hidden(s + 1)
+            if 7 in off:
+                pool_gain(off[7])
+            if 8 in off:
+                pool_turn(off[8])
+            if 9 in off:
+                head_out(off[9])
+            if turning:
+                if c <= 3:
+                    tp = turn(b + 1, c)
+                    turn_out(b + 1, c, tp, 0)
                 if c == 1:
-                    tp = turn(b + 1, 2)
-                    turn_out(b + 1, 2, tp, 0)
-                if c == 3:
                     gains(b + 1, 0, 2)
                 if c == 4:
                     gains(b + 1, 2, 4)
                 if c == 5:
-                    gains(b + 1, 4, 7)
-            if c == 2 and 0 <= pb < NBT:
-                tp = spread_b(pb)
-                spread_c(pb, tp)
-            if c == 5 and 0 <= pb < NBT:
-                add_up(pb, 0)
-            if c == 0 and 0 <= b - 2 < NBT:
-                add_up(b - 2, 1)
-            if c == 1 and 0 <= b - 2 < NBT:
-                pool_quant(b - 2)
-            if c == 2 and 0 <= b - 2 < NBT:
-                head_out(b - 2)
+                    gains(b + 1, 4, 6)
+                if c == 6:
+                    gains(b + 1, 6, 7)
             if s == 0:
                 load_v(2, [(0, 8)])
-            if s == 3:
+            if s == 4:
                 load_v(3, [(0, 8)])
-            if s == 14:
+            if s == 15:
                 load_vd(2)
-            if s == 21:
+            if s == 22:
                 load_vd(3)
             if s < 4:
                 nc.scalar.activation(

@@ -80,7 +80,7 @@ def tile_afmpairattentionpooling_kernel(tc, v, ga, wa, ba, h, gp, wp_bytes, wp_s
         pool_c = {}
         pool_s = {}
         wt = {}
-        al = {}
+        inv = {}
         mn_t = {}
         den_t = {}
 
@@ -94,7 +94,7 @@ def tile_afmpairattentionpooling_kernel(tc, v, ga, wa, ba, h, gp, wp_bytes, wp_s
             for i in range(FI):
                 nc.gpsimd.memset(t[:, i, 0 : i + 1], MASKED)
             neg.append(t)
-        junk = keep.tile([P, P], BF16, name="junk")
+        junk = [keep.tile([P, P], BF16, name="junk%d" % n) for n in range(4)]
 
         def load_v(b, pieces):
             vn[b] = work.tile([P, F, D], BF16, name="vn", tag="vn", bufs=2)
@@ -123,9 +123,9 @@ def tile_afmpairattentionpooling_kernel(tc, v, ga, wa, ba, h, gp, wp_bytes, wp_s
         nc.sync.dma_start(out=gp_r[:], in_=gp.partition_broadcast(P))
         wps = keep.tile([P, 4], F32, name="wps")
         nc.sync.dma_start(out=wps[:], in_=wp_scale.rearrange("(p t) o -> p (t o)", t=4))
-        load_v(1, [(0, 8)])
         wpb = keep.tile([P, 4, O], U8, name="wpb")
         nc.sync.dma_start(out=wpb[:], in_=wp_bytes.rearrange("(p t) o -> p t o", t=4))
+        load_v(1, [(0, 8)])
         load_vd(0)
         load_vd(1)
 
@@ -153,18 +153,20 @@ def tile_afmpairattentionpooling_kernel(tc, v, ga, wa, ba, h, gp, wp_bytes, wp_s
 
         def gains(b, i0, i1):
             if b not in vg:
-                vg[b] = work.tile([P, 4, FI, P], F32, name="vg", tag="vg", bufs=2, align_bytes=64)
-            for t in range(4):
-                nc.scalar.activation(
-                    out=vg[b][:, t, i0:i1, :], in_=vT[b][:, i0:i1, :, t], func=ACT.Copy, scale=ga_f[:, t : t + 1]
-                )
+                vg[b] = work.tile([P, FI, P, 4], F32, name="vg", tag="vg", bufs=2, align_bytes=64)
+            nc.vector.tensor_tensor(
+                out=vg[b][:, i0:i1],
+                in0=vT[b][:, i0:i1],
+                in1=ga_b[:].unsqueeze(1).unsqueeze(1).to_broadcast([P, i1 - i0, P, 4]),
+                op=MULT,
+            )
 
         def products(s):
             b, c = divmod(s, NCH)
             eg[s] = work.tile([P, 4, P, 4], BF16, name="eg", tag="eg", bufs=3, align_bytes=64)
             o = 0
             for i, j0, n in chunk(b, c):
-                left = vg[b][:, :, i, :].rearrange("p t b -> p b t").unsqueeze(1).to_broadcast([P, n, P, 4])
+                left = vg[b][:, i].unsqueeze(1).to_broadcast([P, n, P, 4])
                 nc.vector.tensor_tensor(out=eg[s][:, o : o + n], in0=left, in1=vT[b][:, j0 : j0 + n], op=MULT)
                 o += n
 
@@ -191,14 +193,15 @@ def tile_afmpairattentionpooling_kernel(tc, v, ga, wa, ba, h, gp, wp_bytes, wp_s
                 )
 
         def on_vector(s, a):
-            return a == 3 or (a == 2 and s % 3 != 2)
+            return a == 3
 
-        def weigh_s(s):
+        def weigh_s(s, between):
             mine = [a for a in range(4) if not on_vector(s, a)]
             for a in mine:
                 nc.scalar.activation(
                     out=zt[s][:, a, :], in_=mxs[s, a][:], func=ACT.Relu, bias=ba_f[:, a : a + 1], scale=1.0
                 )
+            between()
             for a in mine:
                 nc.scalar.activation(
                     out=zt[s][:, a, :], in_=zt[s][:, a, :], func=ACT.Identity, bias=nhba[:, a : a + 1],
@@ -214,7 +217,7 @@ def tile_afmpairattentionpooling_kernel(tc, v, ga, wa, ba, h, gp, wp_bytes, wp_s
                     )
 
         def scores(s):
-            ut[s] = psum.tile([P, 4, P], F32, name="ut", tag="ut", bufs=1)
+            ut[s] = psum.tile([P, 4, P], F32, name="ut", tag="ut", bufs=2)
             for q in range(4):
                 for a in range(4):
                     nc.tensor.matmul(
@@ -232,7 +235,7 @@ def tile_afmpairattentionpooling_kernel(tc, v, ga, wa, ba, h, gp, wp_bytes, wp_s
             for i, j0, n in chunk(b, c):
                 for j in range(j0, j0 + n):
                     nc.scalar.activation(
-                        out=junk[:], in_=ut[s][:, q, :], func=ACT.Copy, scale=-1.0, accum_out=neg[b % 2][:, i, j : j + 1]
+                        out=junk[q][:], in_=ut[s][:, q, :], func=ACT.Copy, scale=-1.0, accum_out=neg[b % 2][:, i, j : j + 1]
                     )
                     q += 1
 
@@ -249,13 +252,13 @@ def tile_afmpairattentionpooling_kernel(tc, v, ga, wa, ba, h, gp, wp_bytes, wp_s
             )
 
         def soft_d(b):
-            inv = work.tile([P, 1], F32, name="inv", tag="inv")
-            nc.vector.reciprocal(out=inv[:], in_=den_t[b][:])
             hl[b] = work.tile([P, FI, 2, F], BF16, name="hl", tag="hl")
-            al[b] = work.tile([P, FI, F], F32, name="al", tag="al")
-            nc.vector.tensor_scalar(out=al[b][:], in0=pe[b][:], scalar1=inv[:], scalar2=None, op0=MULT)
-            nc.vector.tensor_copy(out=hl[b][:, :, 0, :], in_=al[b][:])
-            nc.vector.tensor_tensor(out=hl[b][:, :, 1, :], in0=al[b][:], in1=hl[b][:, :, 0, :], op=SUB)
+            nc.vector.tensor_copy(out=hl[b][:, :, 0, :], in_=pe[b][:])
+            nc.vector.tensor_tensor(out=hl[b][:, :, 1, :], in0=pe[b][:], in1=hl[b][:, :, 0, :], op=SUB)
+
+        def soft_e(b):
+            inv[b] = work.tile([P, 1], F32, name="inv", tag="inv", bufs=3)
+            nc.vector.reciprocal(out=inv[b][:], in_=den_t[b][:])
 
         def spread_a(b):
             xb[b] = work.tile([P, FI * 2, 8, F], BF16, name="xb", tag="xb")
@@ -302,7 +305,7 @@ def tile_afmpairattentionpooling_kernel(tc, v, ga, wa, ba, h, gp, wp_bytes, wp_s
 
         def add_up(b, t):
             if t == 0:
-                pn[b] = psum.tile([P, 4, P], F32, name="pn", tag="pn", bufs=1)
+                pn[b] = psum.tile([P, 4, P], F32, name="pn", tag="tp", bufs=1)
             for i in range(FI):
                 nc.tensor.matmul(
                     out=pn[b][:, t, :], lhsT=qt[b][:, t, i, :], rhs=id32[:], start=(i == 0), stop=(i == FI - 1),
@@ -311,11 +314,13 @@ def tile_afmpairattentionpooling_kernel(tc, v, ga, wa, ba, h, gp, wp_bytes, wp_s
 
         def pool_gain(b):
             pool_n[b] = work.tile([P, P, 4], BF16, name="pool_n", tag="pool_n")
-            nc.vector.tensor_tensor(
+            nc.vector.scalar_tensor_tensor(
                 out=pool_n[b][:],
                 in0=pn[b][:].rearrange("b t p -> b p t"),
+                scalar=inv[b][:],
                 in1=gp_r[:].rearrange("b (p t) -> b p t", t=4),
-                op=MULT,
+                op0=MULT,
+                op1=MULT,
             )
 
         def pool_turn(b):
@@ -350,17 +355,18 @@ def tile_afmpairattentionpooling_kernel(tc, v, ga, wa, ba, h, gp, wp_bytes, wp_s
                 nc.scalar.copy(out=osb[:, cols], in_=mx[:])
                 nc.sync.dma_start(out=out[b * P : (b + 1) * P, cols], in_=osb[:, cols])
 
-        ga_f = keep.tile([P, 4], F32, name="ga_f")
-        nc.gpsimd.tensor_copy(out=ga_f[:], in_=ga_b[:])
-        for m in range(4):
-            tp = turn(0, m)
-            turn_out(0, m, tp, m == 1)
-            if m == 0:
-                gains(0, 0, 2)
-        products(0)
-        gains(0, 2, 7)
         wa_g = keep.tile([P, A, 4], BF16, name="wa_g", align_bytes=64)
-        nc.vector.tensor_copy(out=wa_g[:], in_=wa_raw[:].rearrange("p j a -> p a j"))
+        tp = turn(0, 0)
+        turn_out(0, 0, tp, 0)
+        gains(0, 0, 2)
+        tp = turn(0, 1)
+        turn_out(0, 1, tp, 1)
+        nc.scalar.copy(out=wa_g[:], in_=wa_raw[:].rearrange("p j a -> p a j"))
+        products(0)
+        tp = turn(0, 2)
+        turn_out(0, 2, tp, 0)
+        tp = turn(0, 3)
+        turn_out(0, 3, tp, 0)
         quantize(0)
         wa_codes = keep.tile([P, A], U32, name="wa_codes", align_bytes=64)
         wa_planes = keep.tile([P, A], U8, name="wa_planes", align_bytes=64)
@@ -368,10 +374,6 @@ def tile_afmpairattentionpooling_kernel(tc, v, ga, wa, ba, h, gp, wp_bytes, wp_s
             out=wa_codes[:].bitcast(FP8X4), scales=wa_planes[:], in_=wa_g[:].rearrange("p a j -> p (a j)")
         )
         mask = keep.tile([P, 8], BF16, name="mask")
-        with nc.allow_low_precision(reason="sums of zeros and a single one"):
-            nc.vector.tensor_reduce(
-                out=mask[:], in_=idb[:].rearrange("p (h r j) -> p r h j", h=2, r=8), axis=AX.XY, op=ADD
-            )
         ba_f = keep.tile([P, 4], F32, name="ba_f")
         nc.gpsimd.tensor_copy(out=ba_f[:], in_=ba_b[:, :, 0])
         h_f = keep.tile([P, 4], F32, name="h_f")
@@ -381,14 +383,25 @@ def tile_afmpairattentionpooling_kernel(tc, v, ga, wa, ba, h, gp, wp_bytes, wp_s
         nhba = keep.tile([P, 4], F32, name="nhba")
         nc.gpsimd.tensor_tensor(out=nhba[:], in0=h_f[:], in1=nba[:], op=MULT)
         hidden(0)
+        gains(0, 2, 4)
         products(1)
+        with nc.allow_low_precision(reason="sums of zeros and a single one"):
+            nc.vector.tensor_reduce(
+                out=mask[:], in_=idb[:].rearrange("p (h r j) -> p r h j", h=2, r=8), axis=AX.XY, op=ADD
+            )
+        gains(0, 4, 7)
 
         wpl = keep.tile([P, 4, O], BF16, name="wpl")
         wpg = keep.tile([P, O, 4], BF16, name="wpg", align_bytes=64)
         wp_codes = keep.tile([P, O], U32, name="wp_codes", align_bytes=64)
         wp_planes = keep.tile([P, O], U8, name="wp_planes", align_bytes=64)
 
-        tail = 10
+        for t in range(4):
+            nc.scalar.activation(
+                out=wpl[:, t, :], in_=wpb[:, t, :].bitcast(E4M3), func=ACT.Copy, scale=wps[:, t : t + 1]
+            )
+        tail = 4
+        turned = {}
         for s in range(NSLOT + tail):
             b, c = divmod(s, NCH)
             live = s < NSLOT
@@ -402,49 +415,70 @@ def tile_afmpairattentionpooling_kernel(tc, v, ga, wa, ba, h, gp, wp_bytes, wp_s
 
             if 2 <= s <= NSLOT + 1:
                 sums(s - 2)
+            def between():
+                if live and b + 1 < NBT and 1 <= c <= 4:
+                    turn_out(b + 1, c - 1, turned[b + 1, c - 1], 0)
+
             if live:
-                weigh_s(s)
+                weigh_s(s, between)
                 weigh_v(s)
+            if 3 in off:
+                spread_c(off[3], turned[off[3]])
             if 1 in off:
                 soft_b(off[1])
                 soft_c(off[1])
-            if 2 in off:
-                tp = spread_b(off[2])
-                spread_c(off[2], tp)
-            for t in range(4):
-                if t + 3 in off:
-                    weigh(off[t + 3], 0, t)
-                    weigh_out(off[t + 3], 0, t)
-                if t + 4 in off:
-                    add_up(off[t + 4], t)
             if 1 <= s <= NSLOT:
                 scores(s - 1)
+            last = 3 in off and off[3] == NBT - 1
+            tt = [t for t in range(4) if t + 3 in off and off[t + 3] < NBT - 1]
+            ta = [t for t in range(4) if t + 4 in off and off[t + 4] < NBT - 1]
+            for t in tt:
+                weigh(off[t + 3], 0, t)
             if s + 1 < NSLOT:
                 quantize(s + 1)
-            if 9 in off:
-                pool_quant(off[9])
             if 1 in off:
                 soft_d(off[1])
                 spread_a(off[1])
-            if s + 2 < NSLOT:
-                products(s + 2)
-            for t in range(4):
-                if t + 3 in off:
-                    weigh(off[t + 3], 1, t)
-                    weigh_out(off[t + 3], 1, t)
+            for t in tt:
+                weigh_out(off[t + 3], 0, t)
+                weigh(off[t + 3], 1, t)
             if s + 1 < NSLOT:
                 hidden(s + 1)
-            if 7 in off:
+            for t in ta:
+                add_up(off[t + 4], t)
+            if s + 2 < NSLOT:
+                products(s + 2)
+            if 1 in off:
+                soft_e(off[1])
+            for t in tt:
+                weigh_out(off[t + 3], 1, t)
+            if 7 in off and off[7] < NBT - 1:
                 pool_gain(off[7])
-            if 8 in off:
+            if 8 in off and off[8] < NBT - 1:
                 pool_turn(off[8])
-            if 9 in off:
+            if 9 in off and off[9] < NBT - 1:
+                pool_quant(off[9])
                 head_out(off[9])
+            if 2 in off:
+                turned[off[2]] = spread_b(off[2])
+            if last:
+                z = NBT - 1
+                for t in range(4):
+                    weigh(z, 0, t)
+                    weigh(z, 1, t)
+                    weigh_out(z, 0, t)
+                    weigh_out(z, 1, t)
+                    if t > 0:
+                        add_up(z, t - 1)
+                add_up(z, 3)
+                pool_gain(z)
+                pool_turn(z)
+                pool_quant(z)
+                head_out(z)
             if turning:
                 if c <= 3:
-                    tp = turn(b + 1, c)
-                    turn_out(b + 1, c, tp, 0)
-                if c == 1:
+                    turned[b + 1, c] = turn(b + 1, c)
+                if c == 3:
                     gains(b + 1, 0, 2)
                 if c == 4:
                     gains(b + 1, 2, 4)
@@ -460,7 +494,7 @@ def tile_afmpairattentionpooling_kernel(tc, v, ga, wa, ba, h, gp, wp_bytes, wp_s
                 load_vd(2)
             if s == 22:
                 load_vd(3)
-            if s < 4:
+            if s < 0:
                 nc.scalar.activation(
                     out=wpl[:, s, :], in_=wpb[:, s, :].bitcast(E4M3), func=ACT.Copy, scale=wps[:, s : s + 1]
                 )

@@ -24,30 +24,24 @@ P = 128
 NBT = B // P
 FI = F - 1
 CHUNKS = [
-    [(0, 1, 4)],
-    [(1, 2, 4)],
-    [(2, 3, 4)],
-    [(3, 4, 4)],
-    [(0, 5, 3), (2, 7, 1)],
-    [(4, 5, 3), (6, 7, 1)],
-    [(1, 6, 2), (5, 6, 2)],
-]
-CHUNKS_FIRST = [
-    [(0, 1, 3), (1, 2, 1)],
-    [(1, 3, 2), (2, 3, 2)],
-    [(0, 4, 4)],
-    [(1, 5, 3), (2, 5, 1)],
-    [(2, 6, 2), (3, 4, 2)],
-    [(3, 6, 2), (4, 5, 2)],
-    [(4, 7, 1), (5, 6, 2), (6, 7, 1)],
+    ([(0, 1, 2)], [(0, 3, 2)]),
+    ([(0, 5, 3)], [(1, 2, 1)]),
+    ([(1, 3, 2)], [(1, 5, 2)]),
+    ([(1, 7, 1)], [(2, 3, 3)]),
+    ([(2, 6, 2)], [(3, 4, 2)]),
+    ([(3, 6, 2)], [(4, 5, 2)]),
+    ([(4, 7, 1)], [(5, 6, 2), (6, 7, 1)]),
 ]
 NCH = len(CHUNKS)
 NSLOT = NBT * NCH
 MASKED = float(2.0 ** 100)
-
-
-def chunk(b, c):
-    return CHUNKS_FIRST[c] if b == 0 else CHUNKS[c]
+VEC2 = ()
+SV = (2, 3, 4,)
+SGS = (1, 4,)
+SPLIT = True
+MXB = 3
+UTB = 2
+ORDER = "pq mask h3 q z0 z1 u z2 w0 sum z3 sb e0 sc ho se gs h o0 sd g add out gn sv d0 pt spb sa t e1 w1 pg d1 v o1".split()
 
 
 def tile_afmpairattentionpooling_kernel(tc, v, ga, wa, ba, h, gp, wp_bytes, wp_scale, out):
@@ -59,42 +53,24 @@ def tile_afmpairattentionpooling_kernel(tc, v, ga, wa, ba, h, gp, wp_bytes, wp_s
         ctx.enter_context(nc.allow_non_contiguous_dma(reason="vectors of 512 onto the partitions"))
         ctx.enter_context(tc.manual_schedule())
 
-        vn = {}
-        vd = {}
-        vT = {}
-        vg = {}
-        eg = {}
-        codes = {}
-        planes = {}
-        zt = {}
-        mxs = {}
-        ut = {}
-        hl = {}
-        pe = {}
-        xb = {}
-        am = {}
-        qt = {}
-        pool_b = {}
-        pool_n = {}
-        pn = {}
-        pool_c = {}
-        pool_s = {}
-        wt = {}
-        inv = {}
-        mn_t = {}
-        den_t = {}
+        vn, vd, vT, vg, vgp, eg, codes, planes = {}, {}, {}, {}, {}, {}, {}, {}
+        zt, mxs, ut, pe, den, mn, inv, hl, xb, am, wt, qt, pn = {}, {}, {}, {}, {}, {}, {}, {}, {}, {}, {}, {}, {}
+        pool_n, pool_b, pool_c, pool_s, turned = {}, {}, {}, {}, {}
 
-        id32 = keep.tile([P, P], F32, name="id32")
         idb = keep.tile([P, P], BF16, name="idb")
-        make_identity(nc, id32[:])
+        id32 = keep.tile([P, P], F32, name="id32")
         make_identity(nc, idb[:])
+        make_identity(nc, id32[:])
         neg = []
         for n in range(2):
             t = keep.tile([P, FI, F], F32, name="neg%d" % n)
             for i in range(FI):
                 nc.gpsimd.memset(t[:, i, 0 : i + 1], MASKED)
             neg.append(t)
-        junk = [keep.tile([P, P], BF16, name="junk%d" % n) for n in range(4)]
+        junk = []
+        for n in range(4):
+            t = keep.tile([P, P], BF16, name="junk%d" % n)
+            junk.append(t)
 
         def load_v(b, pieces):
             vn[b] = work.tile([P, F, D], BF16, name="vn", tag="vn", bufs=2)
@@ -107,25 +83,23 @@ def tile_afmpairattentionpooling_kernel(tc, v, ga, wa, ba, h, gp, wp_bytes, wp_s
             for hh in range(2):
                 nc.sync.dma_start(out=vd[b][64 * hh : 64 * hh + 64], in_=src)
 
-        load_v(0, [(0, 2)])
         ga_b = keep.tile([P, 4], BF16, name="ga_b")
         nc.sync.dma_start(out=ga_b[:], in_=ga.rearrange("(p t) -> p t", t=4))
-        nc.sync.dma_start(out=vn[0][:, 2:4, :], in_=v[0:P, 2:4, :])
+        load_v(0, [(0, 2), (2, 4), (4, 6)])
         wa_raw = keep.tile([P, 4, A], BF16, name="wa_raw")
         nc.sync.dma_start(out=wa_raw[:], in_=wa.rearrange("(p j) a -> p j a", j=4))
-        for f0 in (4, 6):
-            nc.sync.dma_start(out=vn[0][:, f0 : f0 + 2, :], in_=v[0:P, f0 : f0 + 2, :])
+        nc.sync.dma_start(out=vn[0][:, 6:8, :], in_=v[0:P, 6:8, :])
         ba_b = keep.tile([P, 4, 2], BF16, name="ba_b")
         nc.sync.dma_start(out=ba_b[:, :, 0], in_=ba.rearrange("(c p) -> p c", p=P))
         h_b = keep.tile([P, 4, 2], BF16, name="h_b")
         nc.sync.dma_start(out=h_b[:, :, 0], in_=h.rearrange("(c p) -> p c", p=P))
-        gp_r = keep.tile([P, D], BF16, name="gp_r")
-        nc.sync.dma_start(out=gp_r[:], in_=gp.partition_broadcast(P))
         wps = keep.tile([P, 4], F32, name="wps")
         nc.sync.dma_start(out=wps[:], in_=wp_scale.rearrange("(p t) o -> p (t o)", t=4))
         wpb = keep.tile([P, 4, O], U8, name="wpb")
         nc.sync.dma_start(out=wpb[:], in_=wp_bytes.rearrange("(p t) o -> p t o", t=4))
         load_v(1, [(0, 8)])
+        gp_r = keep.tile([P, D], BF16, name="gp_r")
+        nc.sync.dma_start(out=gp_r[:], in_=gp.partition_broadcast(P))
         load_vd(0)
         load_vd(1)
 
@@ -133,7 +107,7 @@ def tile_afmpairattentionpooling_kernel(tc, v, ga, wa, ba, h, gp, wp_bytes, wp_s
             if m == 0:
                 vT[b] = work.tile([P, F, P, 4], BF16, name="vT", tag="vT", bufs=3, align_bytes=64)
             if b == 0:
-                tp = psum.tile([P, 2, 2, P], F32, name="tp", tag="mx", bufs=4)
+                tp = psum.tile([P, 2, 2, P], F32, name="tp", tag="mx", bufs=MXB)
             else:
                 tp = psum.tile([P, 2, 2, P], F32, name="tp", tag="tp", bufs=1)
             words = vn[b][:].bitcast(F32)
@@ -151,23 +125,44 @@ def tile_afmpairattentionpooling_kernel(tc, v, ga, wa, ba, h, gp, wp_bytes, wp_s
             else:
                 nc.vector.tensor_copy(out=dst, in_=src)
 
-        def gains(b, i0, i1):
-            if b not in vg:
-                vg[b] = work.tile([P, FI, P, 4], F32, name="vg", tag="vg", bufs=2, align_bytes=64)
+        def on_pe(b):
+            return 4 if b == 0 else 5
+
+        def gains(b):
+            i0 = on_pe(b)
+            vg[b] = work.tile([P, 3, P, 4], F32, name="vg", tag="vg", bufs=2, align_bytes=64)
             nc.vector.tensor_tensor(
-                out=vg[b][:, i0:i1],
-                in0=vT[b][:, i0:i1],
-                in1=ga_b[:].unsqueeze(1).unsqueeze(1).to_broadcast([P, i1 - i0, P, 4]),
+                out=vg[b][:, 0 : FI - i0],
+                in0=vT[b][:, i0:FI],
+                in1=ga_b[:].unsqueeze(1).unsqueeze(1).to_broadcast([P, FI - i0, P, 4]),
                 op=MULT,
             )
 
-        def products(s):
+        def gain_pe(b, i):
+            if i >= on_pe(b) or (b, i) in vgp:
+                return
+            vgp[b, i] = psum.tile([P, P, 4], F32, name="vgp", tag="vgp", bufs=1)
+            for t in range(4):
+                nc.tensor.matmul(
+                    out=vgp[b, i][:, :, t], lhsT=dg[t][:], rhs=vT[b][:, i, :, t], start=True, stop=True
+                )
+
+        def products(s, part):
             b, c = divmod(s, NCH)
-            eg[s] = work.tile([P, 4, P, 4], BF16, name="eg", tag="eg", bufs=3, align_bytes=64)
-            o = 0
-            for i, j0, n in chunk(b, c):
-                left = vg[b][:, i].unsqueeze(1).to_broadcast([P, n, P, 4])
-                nc.vector.tensor_tensor(out=eg[s][:, o : o + n], in0=left, in1=vT[b][:, j0 : j0 + n], op=MULT)
+            if part == 0:
+                eg[s] = work.tile([P, 4, P, 4], BF16, name="eg", tag="eg", bufs=3, align_bytes=64)
+            o = 0 if part == 0 else sum(n for i, j0, n in CHUNKS[c][0])
+            for i, j0, n in CHUNKS[c][part]:
+                if i < on_pe(b):
+                    left = vgp[b, i][:]
+                else:
+                    left = vg[b][:, i - on_pe(b)]
+                nc.vector.tensor_tensor(
+                    out=eg[s][:, o : o + n],
+                    in0=left.unsqueeze(1).to_broadcast([P, n, P, 4]),
+                    in1=vT[b][:, j0 : j0 + n],
+                    op=MULT,
+                )
                 o += n
 
         def quantize(s):
@@ -177,13 +172,13 @@ def tile_afmpairattentionpooling_kernel(tc, v, ga, wa, ba, h, gp, wp_bytes, wp_s
                 out=codes[s][:].bitcast(FP8X4), scales=planes[s][:], in_=eg[s][:].rearrange("p q b t -> p (q b t)")
             )
 
-        def hidden(s):
-            zt[s] = work.tile([P, 4, 512], F32, name="zt", tag="zt", bufs=3)
-            for a in range(4):
-                mx = psum.tile([P, 512], F32, name="mx", tag="mx", bufs=4)
-                mxs[s, a] = mx
+        def hidden(s, blocks):
+            if 0 in blocks:
+                zt[s] = work.tile([P, 4, 512], F32, name="zt", tag="zt", bufs=3)
+            for a in blocks:
+                mxs[s, a] = psum.tile([P, 512], F32, name="mx", tag="mx", bufs=MXB)
                 nc.tensor.matmul_mx(
-                    out=mx[:],
+                    out=mxs[s, a][:],
                     lhsT=wa_codes[:, a * P : (a + 1) * P].bitcast(FP8X4),
                     lhsT_scale=wa_planes[:, a * P : (a + 1) * P],
                     rhs=codes[s][:].bitcast(FP8X4),
@@ -193,20 +188,44 @@ def tile_afmpairattentionpooling_kernel(tc, v, ga, wa, ba, h, gp, wp_bytes, wp_s
                 )
 
         def on_vector(s, a):
-            return a == 3
+            return a == 3 and s % NCH in VEC2
 
-        def weigh_s(s, between):
-            mine = [a for a in range(4) if not on_vector(s, a)]
-            for a in mine:
-                nc.scalar.activation(
-                    out=zt[s][:, a, :], in_=mxs[s, a][:], func=ACT.Relu, bias=ba_f[:, a : a + 1], scale=1.0
-                )
-            between()
-            for a in mine:
-                nc.scalar.activation(
-                    out=zt[s][:, a, :], in_=zt[s][:, a, :], func=ACT.Identity, bias=nhba[:, a : a + 1],
-                    scale=h_f[:, a : a + 1],
-                )
+        def sign_on_vector(s, a):
+            return a == 0 and s % NCH in SV
+
+        def relu_s(s, blocks):
+            for a in blocks:
+                if not on_vector(s, a):
+                    nc.scalar.activation(
+                        out=zt[s][:, a, :], in_=mxs[s, a][:], func=ACT.Relu, bias=ba_f[:, a : a + 1], scale=1.0
+                    )
+
+        def weigh_g(s):
+            for a in range(4):
+                if not on_vector(s, a) and not sign_on_vector(s, a) and not sign_on_scalar(s, a):
+                    nc.gpsimd.tensor_scalar(
+                        out=zt[s][:, a, :], in0=zt[s][:, a, :], scalar1=h_f[:, a : a + 1], scalar2=nhba[:, a : a + 1],
+                        op0=MULT, op1=ADD,
+                    )
+
+        def sign_on_scalar(s, a):
+            return a == 1 and s % NCH in SGS
+
+        def sign_s(s):
+            for a in range(4):
+                if sign_on_scalar(s, a):
+                    nc.scalar.activation(
+                        out=zt[s][:, a, :], in_=zt[s][:, a, :], func=ACT.Identity, bias=nhba[:, a : a + 1],
+                        scale=h_f[:, a : a + 1],
+                    )
+
+        def sign_v(s):
+            for a in range(4):
+                if sign_on_vector(s, a):
+                    nc.vector.tensor_scalar(
+                        out=zt[s][:, a, :], in0=zt[s][:, a, :], scalar1=h_f[:, a : a + 1], scalar2=nhba[:, a : a + 1],
+                        op0=MULT, op1=ADD,
+                    )
 
         def weigh_v(s):
             for a in range(4):
@@ -217,7 +236,7 @@ def tile_afmpairattentionpooling_kernel(tc, v, ga, wa, ba, h, gp, wp_bytes, wp_s
                     )
 
         def scores(s):
-            ut[s] = psum.tile([P, 4, P], F32, name="ut", tag="ut", bufs=2)
+            ut[s] = psum.tile([P, 4, P], F32, name="ut", tag="ut", bufs=UTB)
             for q in range(4):
                 for a in range(4):
                     nc.tensor.matmul(
@@ -232,23 +251,24 @@ def tile_afmpairattentionpooling_kernel(tc, v, ga, wa, ba, h, gp, wp_bytes, wp_s
         def sums(s):
             b, c = divmod(s, NCH)
             q = 0
-            for i, j0, n in chunk(b, c):
-                for j in range(j0, j0 + n):
-                    nc.scalar.activation(
-                        out=junk[q][:], in_=ut[s][:, q, :], func=ACT.Copy, scale=-1.0, accum_out=neg[b % 2][:, i, j : j + 1]
-                    )
-                    q += 1
+            for part in range(2):
+                for i, j0, n in CHUNKS[c][part]:
+                    for j in range(j0, j0 + n):
+                        nc.scalar.activation(
+                            out=junk[q][:], in_=ut[s][:, q, :], func=ACT.Copy, scale=-1.0,
+                            accum_out=neg[b % 2][:, i, j : j + 1],
+                        )
+                        q += 1
 
         def soft_b(b):
-            mn_t[b] = work.tile([P, 1], F32, name="mn", tag="mn")
-            nc.vector.tensor_reduce(out=mn_t[b][:], in_=neg[b % 2][:].rearrange("p i j -> p (i j)"), axis=AX.X, op=MIN)
+            mn[b] = work.tile([P, 1], F32, name="mn", tag="mn")
+            nc.vector.tensor_reduce(out=mn[b][:], in_=neg[b % 2][:].rearrange("p i j -> p (i j)"), axis=AX.X, op=MIN)
 
         def soft_c(b):
             pe[b] = work.tile([P, FI, F], F32, name="pe", tag="pe")
-            den_t[b] = work.tile([P, 1], F32, name="den", tag="den")
+            den[b] = work.tile([P, 1], F32, name="den", tag="den")
             nc.scalar.activation(
-                out=pe[b][:].rearrange("p i j -> p (i j)"), in_=neg[b % 2][:].rearrange("p i j -> p (i j)"), func=ACT.Exp, bias=mn_t[b][:], scale=-1.0,
-                accum_out=den_t[b][:],
+                out=pe[b][:], in_=neg[b % 2][:], func=ACT.Exp, bias=mn[b][:], scale=-1.0, accum_out=den[b][:]
             )
 
         def soft_d(b):
@@ -258,10 +278,10 @@ def tile_afmpairattentionpooling_kernel(tc, v, ga, wa, ba, h, gp, wp_bytes, wp_s
 
         def soft_e(b):
             inv[b] = work.tile([P, 1], F32, name="inv", tag="inv", bufs=3)
-            nc.vector.reciprocal(out=inv[b][:], in_=den_t[b][:])
+            nc.vector.reciprocal(out=inv[b][:], in_=den[b][:])
 
         def spread_a(b):
-            xb[b] = work.tile([P, FI * 2, 8, F], BF16, name="xb", tag="xb")
+            xb[b] = work.tile([P, FI * 2, 8, F], BF16, name="xb", tag="xb", bufs=1)
             src = hl[b][:].rearrange("p i h j -> p (i h) j").unsqueeze(2).to_broadcast([P, FI * 2, 8, F])
             nc.scalar.copy(out=xb[b][:], in_=src)
 
@@ -283,7 +303,7 @@ def tile_afmpairattentionpooling_kernel(tc, v, ga, wa, ba, h, gp, wp_bytes, wp_s
 
         def weigh(b, hh, t):
             if b == NBT - 1:
-                wt[b, hh, t] = psum.tile([P, FI, 64], F32, name="wt", tag="mx", bufs=4)
+                wt[b, hh, t] = psum.tile([P, FI, 64], F32, name="wt", tag="mx", bufs=MXB)
             else:
                 wt[b, hh, t] = psum.tile([P, FI, 64], F32, name="wt", tag="wt", bufs=1)
             for g in range(8):
@@ -342,7 +362,7 @@ def tile_afmpairattentionpooling_kernel(tc, v, ga, wa, ba, h, gp, wp_bytes, wp_s
             osb = work.tile([P, O], F32, name="osb", tag="osb", bufs=2)
             for n in range(2):
                 cols = slice(512 * n, 512 * n + 512)
-                mx = psum.tile([P, 512], F32, name="mx", tag="mx", bufs=4)
+                mx = psum.tile([P, 512], F32, name="mxo", tag="mx", bufs=MXB)
                 nc.tensor.matmul_mx(
                     out=mx[:],
                     lhsT=pool_c[b][:].bitcast(FP8X4),
@@ -352,27 +372,43 @@ def tile_afmpairattentionpooling_kernel(tc, v, ga, wa, ba, h, gp, wp_bytes, wp_s
                     start=True,
                     stop=True,
                 )
-                nc.scalar.copy(out=osb[:, cols], in_=mx[:])
+                if b == NBT - 1 and n == 1:
+                    nc.vector.tensor_copy(out=osb[:, cols], in_=mx[:])
+                else:
+                    nc.scalar.copy(out=osb[:, cols], in_=mx[:])
                 nc.sync.dma_start(out=out[b * P : (b + 1) * P, cols], in_=osb[:, cols])
 
+        dg = []
+        for t in range(4):
+            d = keep.tile([P, P], BF16, name="dg%d" % t)
+            nc.vector.tensor_scalar(out=d[:], in0=idb[:], scalar1=ga_b[:, t : t + 1], scalar2=None, op0=MULT)
+            dg.append(d)
         wa_g = keep.tile([P, A, 4], BF16, name="wa_g", align_bytes=64)
-        tp = turn(0, 0)
-        turn_out(0, 0, tp, 0)
-        gains(0, 0, 2)
-        tp = turn(0, 1)
-        turn_out(0, 1, tp, 1)
-        nc.scalar.copy(out=wa_g[:], in_=wa_raw[:].rearrange("p j a -> p a j"))
-        products(0)
-        tp = turn(0, 2)
-        turn_out(0, 2, tp, 0)
-        tp = turn(0, 3)
-        turn_out(0, 3, tp, 0)
-        quantize(0)
+        tp0 = turn(0, 0)
+        tp1 = turn(0, 1)
+        tp2 = turn(0, 2)
+        turn_out(0, 0, tp0, 0)
+        turn_out(0, 1, tp1, 1)
+        turn_out(0, 2, tp2, 0)
+        gain_pe(0, 0)
+        products(0, 0)
+        for n in range(2):
+            dst = wa_g[:, 256 * n : 256 * n + 256, :]
+            wsrc = wa_raw[:, :, 256 * n : 256 * n + 256].rearrange("p j a -> p a j")
+            if n == 0:
+                nc.scalar.copy(out=dst, in_=wsrc)
+            else:
+                nc.gpsimd.tensor_scalar(out=dst, in0=wsrc, scalar1=1.0, scalar2=0.0, op0=MULT, op1=ADD)
+        products(0, 1)
+        tp3 = turn(0, 3)
+        turn_out(0, 3, tp3, 0)
         wa_codes = keep.tile([P, A], U32, name="wa_codes", align_bytes=64)
         wa_planes = keep.tile([P, A], U8, name="wa_planes", align_bytes=64)
         nc.vector.quantize_mx(
             out=wa_codes[:].bitcast(FP8X4), scales=wa_planes[:], in_=wa_g[:].rearrange("p a j -> p (a j)")
         )
+        quantize(0)
+        products(1, 0)
         mask = keep.tile([P, 8], BF16, name="mask")
         ba_f = keep.tile([P, 4], F32, name="ba_f")
         nc.gpsimd.tensor_copy(out=ba_f[:], in_=ba_b[:, :, 0])
@@ -382,86 +418,106 @@ def tile_afmpairattentionpooling_kernel(tc, v, ga, wa, ba, h, gp, wp_bytes, wp_s
         nc.gpsimd.tensor_scalar(out=nba[:], in0=ba_f[:], scalar1=-1.0, scalar2=None, op0=MULT)
         nhba = keep.tile([P, 4], F32, name="nhba")
         nc.gpsimd.tensor_tensor(out=nhba[:], in0=h_f[:], in1=nba[:], op=MULT)
-        hidden(0)
-        gains(0, 2, 4)
-        products(1)
+        hidden(0, (0, 1, 2) if SPLIT else (0, 1, 2, 3))
+        gain_pe(0, 1)
+        products(1, 1)
         with nc.allow_low_precision(reason="sums of zeros and a single one"):
             nc.vector.tensor_reduce(
                 out=mask[:], in_=idb[:].rearrange("p (h r j) -> p r h j", h=2, r=8), axis=AX.XY, op=ADD
             )
-        gains(0, 4, 7)
 
         wpl = keep.tile([P, 4, O], BF16, name="wpl")
         wpg = keep.tile([P, O, 4], BF16, name="wpg", align_bytes=64)
         wp_codes = keep.tile([P, O], U32, name="wp_codes", align_bytes=64)
         wp_planes = keep.tile([P, O], U8, name="wp_planes", align_bytes=64)
 
-        for t in range(4):
+        def widen(t):
             nc.scalar.activation(
                 out=wpl[:, t, :], in_=wpb[:, t, :].bitcast(E4M3), func=ACT.Copy, scale=wps[:, t : t + 1]
             )
-        tail = 4
-        turned = {}
-        for s in range(NSLOT + tail):
+
+        widen(0)
+        widen(1)
+
+        for s in range(NSLOT + 4):
             b, c = divmod(s, NCH)
             live = s < NSLOT
-            turning = live and b + 1 < NBT
-
             off = {}
             for bb in range(NBT):
                 k = s - NCH * (bb + 1)
                 if 0 <= k <= 12:
                     off[k] = bb
+            wi = [t for t in range(4) if t + 3 in off and off[t + 3] < NBT - 1]
+            ta = [t for t in range(4) if t + 4 in off and off[t + 4] < NBT - 1]
 
-            if 2 <= s <= NSLOT + 1:
-                sums(s - 2)
-            def between():
+            def z_rest():
+                relu_s(s, (1, 2, 3))
+
+            def tout():
                 if live and b + 1 < NBT and 1 <= c <= 4:
                     turn_out(b + 1, c - 1, turned[b + 1, c - 1], 0)
 
-            if live:
-                weigh_s(s, between)
-                weigh_v(s)
-            if 3 in off:
-                spread_c(off[3], turned[off[3]])
-            if 1 in off:
-                soft_b(off[1])
-                soft_c(off[1])
-            if 1 <= s <= NSLOT:
-                scores(s - 1)
-            last = 3 in off and off[3] == NBT - 1
-            tt = [t for t in range(4) if t + 3 in off and off[t + 3] < NBT - 1]
-            ta = [t for t in range(4) if t + 4 in off and off[t + 4] < NBT - 1]
-            for t in tt:
-                weigh(off[t + 3], 0, t)
-            if s + 1 < NSLOT:
-                quantize(s + 1)
-            if 1 in off:
-                soft_d(off[1])
-                spread_a(off[1])
-            for t in tt:
-                weigh_out(off[t + 3], 0, t)
-                weigh(off[t + 3], 1, t)
-            if s + 1 < NSLOT:
-                hidden(s + 1)
-            for t in ta:
-                add_up(off[t + 4], t)
-            if s + 2 < NSLOT:
-                products(s + 2)
-            if 1 in off:
-                soft_e(off[1])
-            for t in tt:
-                weigh_out(off[t + 3], 1, t)
-            if 7 in off and off[7] < NBT - 1:
-                pool_gain(off[7])
-            if 8 in off and off[8] < NBT - 1:
-                pool_turn(off[8])
-            if 9 in off and off[9] < NBT - 1:
-                pool_quant(off[9])
-                head_out(off[9])
-            if 2 in off:
-                turned[off[2]] = spread_b(off[2])
-            if last:
+            def gpe(n, part):
+                if s + n < NSLOT:
+                    for i, j0, m in CHUNKS[(s + n) % NCH][part]:
+                        gain_pe((s + n) // NCH, i)
+
+            def each(ts, f):
+                for t in ts:
+                    f(t)
+
+            def at(k, f, last=False):
+                if k in off and (last or off[k] < NBT - 1):
+                    f(off[k])
+
+            def spb(z):
+                turned[z] = spread_b(z)
+
+            def trn():
+                if live and b + 1 < NBT and c <= 3:
+                    turned[b + 1, c] = turn(b + 1, c)
+
+            items = {
+                "q": lambda: quantize(s + 1) if s + 1 < NSLOT else None,
+                "e0": lambda: products(s + 2, 0) if s + 2 < NSLOT else None,
+                "e1": lambda: products(s + 2, 1) if s + 2 < NSLOT else None,
+                "z0": lambda: relu_s(s, (0,)) if live else None,
+                "z1": lambda: relu_s(s, (1,)) if live else None,
+                "z2": lambda: relu_s(s, (2,)) if live else None,
+                "z3": lambda: relu_s(s, (3,)) if live else None,
+                "g": lambda: weigh_g(s) if live else None,
+                "gs": lambda: sign_s(s) if live else None,
+                "v": lambda: weigh_v(s) if live else None,
+                "h3": lambda: hidden(s, (3,)) if live and SPLIT else None,
+                "h": lambda: hidden(s + 1, (0, 1, 2) if SPLIT else (0, 1, 2, 3)) if s + 1 < NSLOT else None,
+                "sum": lambda: sums(s - 2) if 2 <= s <= NSLOT + 1 else None,
+                "out": tout,
+                "sb": lambda: at(1, soft_b, True),
+                "sc": lambda: at(1, soft_c, True),
+                "sd": lambda: at(1, soft_d, True),
+                "sa": lambda: at(1, spread_a, True),
+                "se": lambda: at(1, soft_e, True),
+                "mask": lambda: at(3, lambda z: spread_c(z, turned[z]), True),
+                "u": lambda: scores(s - 1) if 1 <= s <= NSLOT else None,
+                "w0": lambda: each(wi, lambda t: weigh(off[t + 3], 0, t)),
+                "o0": lambda: each(wi, lambda t: weigh_out(off[t + 3], 0, t)),
+                "w1": lambda: each(wi, lambda t: weigh(off[t + 3], 1, t)),
+                "o1": lambda: each(wi, lambda t: weigh_out(off[t + 3], 1, t)),
+                "d1": lambda: gpe(2, 1),
+                "d0": lambda: gpe(3, 0),
+                "sv": lambda: sign_v(s) if live else None,
+                "add": lambda: each(ta, lambda t: add_up(off[t + 4], t)),
+                "pg": lambda: at(7, pool_gain),
+                "pt": lambda: at(8, pool_turn),
+                "pq": lambda: at(9, pool_quant),
+                "ho": lambda: at(9, head_out),
+                "spb": lambda: at(2, spb, True),
+                "gn": lambda: gains(b) if live and c == 1 else None,
+                "t": trn,
+            }
+            for name in ORDER:
+                items[name]()
+            if 3 in off and off[3] == NBT - 1:
                 z = NBT - 1
                 for t in range(4):
                     weigh(z, 0, t)
@@ -475,17 +531,6 @@ def tile_afmpairattentionpooling_kernel(tc, v, ga, wa, ba, h, gp, wp_bytes, wp_s
                 pool_turn(z)
                 pool_quant(z)
                 head_out(z)
-            if turning:
-                if c <= 3:
-                    turned[b + 1, c] = turn(b + 1, c)
-                if c == 3:
-                    gains(b + 1, 0, 2)
-                if c == 4:
-                    gains(b + 1, 2, 4)
-                if c == 5:
-                    gains(b + 1, 4, 6)
-                if c == 6:
-                    gains(b + 1, 6, 7)
             if s == 0:
                 load_v(2, [(0, 8)])
             if s == 4:
@@ -494,10 +539,8 @@ def tile_afmpairattentionpooling_kernel(tc, v, ga, wa, ba, h, gp, wp_bytes, wp_s
                 load_vd(2)
             if s == 22:
                 load_vd(3)
-            if s < 0:
-                nc.scalar.activation(
-                    out=wpl[:, s, :], in_=wpb[:, s, :].bitcast(E4M3), func=ACT.Copy, scale=wps[:, s : s + 1]
-                )
+            if s in (0, 1):
+                widen(s + 2)
             if 7 <= s < 11:
                 n0 = 256 * (s - 7)
                 nc.scalar.copy(

@@ -35,13 +35,18 @@ CHUNKS = [
 NCH = len(CHUNKS)
 NSLOT = NBT * NCH
 MASKED = float(2.0 ** 100)
-VEC2 = ()
-SV = (2, 3, 4,)
-SGS = (1, 4,)
+VEC2 = (3,)
+SV = (0, 2, 3, 5,)
+LE = 3
+LQ = 1
+LU = 1
+TO = 0
+WK = [(3, 4, 5, 6, 7, 8, 9, 10), (3, 4, 5, 6, 7, 8, 9, 9), (3, 3, 4, 4, 5, 5, 6, 6)]
+SGS = (1, 2, 3, 4,)
 SPLIT = True
 MXB = 3
 UTB = 2
-ORDER = "pq mask h3 q z0 z1 u z2 w0 sum z3 sb e0 sc ho se gs h o0 sd g add out gn sv d0 pt spb sa t e1 w1 pg d1 v o1".split()
+ORDER = "pq h3 mask z0 q v z1 z2 sum z3 u sb pt w0 ho e0 h add sc out se gs sv sd gn d0 d1 spb o0 sa w1 e1 pg o1 g t".split()
 
 
 def tile_afmpairattentionpooling_kernel(tc, v, ga, wa, ba, h, gp, wp_bytes, wp_scale, out):
@@ -105,7 +110,7 @@ def tile_afmpairattentionpooling_kernel(tc, v, ga, wa, ba, h, gp, wp_bytes, wp_s
 
         def turn(b, m):
             if m == 0:
-                vT[b] = work.tile([P, F, P, 4], BF16, name="vT", tag="vT", bufs=3, align_bytes=64)
+                vT[b] = work.tile([P, F, P, 4], BF16, name="vT", tag="vT", bufs=4, align_bytes=64)
             if b == 0:
                 tp = psum.tile([P, 2, 2, P], F32, name="tp", tag="mx", bufs=MXB)
             else:
@@ -150,7 +155,7 @@ def tile_afmpairattentionpooling_kernel(tc, v, ga, wa, ba, h, gp, wp_bytes, wp_s
         def products(s, part):
             b, c = divmod(s, NCH)
             if part == 0:
-                eg[s] = work.tile([P, 4, P, 4], BF16, name="eg", tag="eg", bufs=3, align_bytes=64)
+                eg[s] = work.tile([P, 4, P, 4], BF16, name="eg", tag="eg", bufs=4, align_bytes=64)
             o = 0 if part == 0 else sum(n for i, j0, n in CHUNKS[c][0])
             for i, j0, n in CHUNKS[c][part]:
                 if i < on_pe(b):
@@ -277,7 +282,7 @@ def tile_afmpairattentionpooling_kernel(tc, v, ga, wa, ba, h, gp, wp_bytes, wp_s
             nc.vector.tensor_tensor(out=hl[b][:, :, 1, :], in0=pe[b][:], in1=hl[b][:, :, 0, :], op=SUB)
 
         def soft_e(b):
-            inv[b] = work.tile([P, 1], F32, name="inv", tag="inv", bufs=3)
+            inv[b] = work.tile([P, 1], F32, name="inv", tag="inv", bufs=4)
             nc.vector.reciprocal(out=inv[b][:], in_=den[b][:])
 
         def spread_a(b):
@@ -286,14 +291,14 @@ def tile_afmpairattentionpooling_kernel(tc, v, ga, wa, ba, h, gp, wp_bytes, wp_s
             nc.scalar.copy(out=xb[b][:], in_=src)
 
         def spread_b(b):
-            tp = psum.tile([P, FI, P], BF16, name="tpb", tag="tp", bufs=1)
+            tp = psum.tile([P, FI, P], BF16, name="tpb", tag="wt" if b == NBT - 1 else "tp", bufs=1)
             flat = xb[b][:].rearrange("p x r j -> p (x r j)")
             for i in range(FI):
                 nc.tensor.transpose(tp[:, i, :], flat[:, i * P : (i + 1) * P], idb[:])
             return tp
 
         def spread_c(b, tp):
-            am[b] = work.tile([P, 16, FI, 8], BF16, name="am", tag="am")
+            am[b] = work.tile([P, 16, FI, 8], BF16, name="am", tag="am", bufs=3)
             nc.vector.tensor_tensor(
                 out=am[b][:].rearrange("m g i r -> m i g r"),
                 in0=tp[:].rearrange("m i (g r) -> m i g r", r=8),
@@ -317,7 +322,7 @@ def tile_afmpairattentionpooling_kernel(tc, v, ga, wa, ba, h, gp, wp_bytes, wp_s
 
         def weigh_out(b, hh, t):
             if b not in qt:
-                qt[b] = work.tile([P, 4, FI, P], F32, name="qt", tag="qt", bufs=1)
+                qt[b] = work.tile([P, 4, FI, P], F32, name="qt", tag="qt", bufs=2)
             cols = slice(64 * hh, 64 * hh + 64)
             nc.vector.tensor_tensor(
                 out=qt[b][:, t, :, cols], in0=wt[b, hh, t][:], in1=vT[b][:, 0:FI, cols, t], op=MULT
@@ -421,6 +426,9 @@ def tile_afmpairattentionpooling_kernel(tc, v, ga, wa, ba, h, gp, wp_bytes, wp_s
         hidden(0, (0, 1, 2) if SPLIT else (0, 1, 2, 3))
         gain_pe(0, 1)
         products(1, 1)
+        gain_pe(0, 1)
+        products(2, 0)
+        products(2, 1)
         with nc.allow_low_precision(reason="sums of zeros and a single one"):
             nc.vector.tensor_reduce(
                 out=mask[:], in_=idb[:].rearrange("p (h r j) -> p r h j", h=2, r=8), axis=AX.XY, op=ADD
@@ -439,23 +447,30 @@ def tile_afmpairattentionpooling_kernel(tc, v, ga, wa, ba, h, gp, wp_bytes, wp_s
         widen(0)
         widen(1)
 
-        for s in range(NSLOT + 4):
+        for s in range(NSLOT):
             b, c = divmod(s, NCH)
             live = s < NSLOT
             off = {}
             for bb in range(NBT):
-                k = s - NCH * (bb + 1)
+                k = s - NCH * (bb + 1) - (LU - 1)
                 if 0 <= k <= 12:
                     off[k] = bb
-            wi = [t for t in range(4) if t + 3 in off and off[t + 3] < NBT - 1]
-            ta = [t for t in range(4) if t + 4 in off and off[t + 4] < NBT - 1]
+            wi = []
+            ta = []
+            for bb in range(NBT - 1):
+                k = s - NCH * (bb + 1) - (LU - 1)
+                for n in range(8):
+                    if k == WK[bb][n]:
+                        wi.append((bb, n % 2, n // 2))
+                if k == WK[bb][7] + 1:
+                    ta.append(bb)
 
             def z_rest():
                 relu_s(s, (1, 2, 3))
 
             def tout():
-                if live and b + 1 < NBT and 1 <= c <= 4:
-                    turn_out(b + 1, c - 1, turned[b + 1, c - 1], 0)
+                if live and b + 1 < NBT and 1 <= c - TO <= 4:
+                    turn_out(b + 1, c - TO - 1, turned[b + 1, c - TO - 1], 0)
 
             def gpe(n, part):
                 if s + n < NSLOT:
@@ -470,17 +485,22 @@ def tile_afmpairattentionpooling_kernel(tc, v, ga, wa, ba, h, gp, wp_bytes, wp_s
                 if k in off and (last or off[k] < NBT - 1):
                     f(off[k])
 
+            def stage(n, f):
+                for bb in range(NBT - 1):
+                    if s - NCH * (bb + 1) - (LU - 1) == n + WK[bb][7] + 1:
+                        f(bb)
+
             def spb(z):
                 turned[z] = spread_b(z)
 
             def trn():
-                if live and b + 1 < NBT and c <= 3:
-                    turned[b + 1, c] = turn(b + 1, c)
+                if live and b + 1 < NBT and 0 <= c - TO <= 3:
+                    turned[b + 1, c - TO] = turn(b + 1, c - TO)
 
             items = {
-                "q": lambda: quantize(s + 1) if s + 1 < NSLOT else None,
-                "e0": lambda: products(s + 2, 0) if s + 2 < NSLOT else None,
-                "e1": lambda: products(s + 2, 1) if s + 2 < NSLOT else None,
+                "q": lambda: quantize(s + LQ) if s + LQ < NSLOT else None,
+                "e0": lambda: products(s + LE, 0) if s + LE < NSLOT else None,
+                "e1": lambda: products(s + LE, 1) if s + LE < NSLOT else None,
                 "z0": lambda: relu_s(s, (0,)) if live else None,
                 "z1": lambda: relu_s(s, (1,)) if live else None,
                 "z2": lambda: relu_s(s, (2,)) if live else None,
@@ -490,7 +510,7 @@ def tile_afmpairattentionpooling_kernel(tc, v, ga, wa, ba, h, gp, wp_bytes, wp_s
                 "v": lambda: weigh_v(s) if live else None,
                 "h3": lambda: hidden(s, (3,)) if live and SPLIT else None,
                 "h": lambda: hidden(s + 1, (0, 1, 2) if SPLIT else (0, 1, 2, 3)) if s + 1 < NSLOT else None,
-                "sum": lambda: sums(s - 2) if 2 <= s <= NSLOT + 1 else None,
+                "sum": lambda: sums(s - LU - 1) if 0 <= s - LU - 1 < NSLOT else None,
                 "out": tout,
                 "sb": lambda: at(1, soft_b, True),
                 "sc": lambda: at(1, soft_c, True),
@@ -498,46 +518,32 @@ def tile_afmpairattentionpooling_kernel(tc, v, ga, wa, ba, h, gp, wp_bytes, wp_s
                 "sa": lambda: at(1, spread_a, True),
                 "se": lambda: at(1, soft_e, True),
                 "mask": lambda: at(3, lambda z: spread_c(z, turned[z]), True),
-                "u": lambda: scores(s - 1) if 1 <= s <= NSLOT else None,
-                "w0": lambda: each(wi, lambda t: weigh(off[t + 3], 0, t)),
-                "o0": lambda: each(wi, lambda t: weigh_out(off[t + 3], 0, t)),
-                "w1": lambda: each(wi, lambda t: weigh(off[t + 3], 1, t)),
-                "o1": lambda: each(wi, lambda t: weigh_out(off[t + 3], 1, t)),
-                "d1": lambda: gpe(2, 1),
-                "d0": lambda: gpe(3, 0),
+                "u": lambda: scores(s - LU) if 0 <= s - LU < NSLOT else None,
+                "w0": lambda: each(wi[0:1], lambda z: weigh(*z)),
+                "o0": lambda: each(wi[0:1], lambda z: weigh_out(*z)),
+                "w1": lambda: each(wi[1:2], lambda z: weigh(*z)),
+                "o1": lambda: each(wi[1:2], lambda z: weigh_out(*z)),
+                "d1": lambda: gpe(LE, 1),
+                "d0": lambda: gpe(LE + 1, 0),
                 "sv": lambda: sign_v(s) if live else None,
-                "add": lambda: each(ta, lambda t: add_up(off[t + 4], t)),
-                "pg": lambda: at(7, pool_gain),
-                "pt": lambda: at(8, pool_turn),
-                "pq": lambda: at(9, pool_quant),
-                "ho": lambda: at(9, head_out),
+                "add": lambda: each(ta, lambda z: each(range(4), lambda t: add_up(z, t))),
+                "pg": lambda: stage(0, pool_gain),
+                "pt": lambda: stage(1, pool_turn),
+                "pq": lambda: stage(2, pool_quant),
+                "ho": lambda: stage(2, head_out),
                 "spb": lambda: at(2, spb, True),
                 "gn": lambda: gains(b) if live and c == 1 else None,
                 "t": trn,
             }
             for name in ORDER:
                 items[name]()
-            if 3 in off and off[3] == NBT - 1:
-                z = NBT - 1
-                for t in range(4):
-                    weigh(z, 0, t)
-                    weigh(z, 1, t)
-                    weigh_out(z, 0, t)
-                    weigh_out(z, 1, t)
-                    if t > 0:
-                        add_up(z, t - 1)
-                add_up(z, 3)
-                pool_gain(z)
-                pool_turn(z)
-                pool_quant(z)
-                head_out(z)
             if s == 0:
                 load_v(2, [(0, 8)])
             if s == 4:
                 load_v(3, [(0, 8)])
-            if s == 15:
+            if s == 18:
                 load_vd(2)
-            if s == 22:
+            if s == 25:
                 load_vd(3)
             if s in (0, 1):
                 widen(s + 2)
@@ -550,3 +556,35 @@ def tile_afmpairattentionpooling_kernel(tc, v, ga, wa, ba, h, gp, wp_bytes, wp_s
                 nc.vector.quantize_mx(
                     out=wp_codes[:].bitcast(FP8X4), scales=wp_planes[:], in_=wpg[:].rearrange("p n j -> p (n j)")
                 )
+
+        y, z = NBT - 2, NBT - 1
+        sums(NSLOT - 2)
+        scores(NSLOT - 1)
+        for t in range(4):
+            add_up(y, t)
+        sums(NSLOT - 1)
+        soft_b(z)
+        soft_c(z)
+        soft_d(z)
+        spread_a(z)
+        pool_gain(y)
+        soft_e(z)
+        tp = spread_b(z)
+        pool_turn(y)
+        spread_c(z, tp)
+        pool_quant(y)
+        for t0 in (0, 2):
+            for hh in range(2):
+                for t in (t0, t0 + 1):
+                    weigh(z, hh, t)
+                    weigh_out(z, hh, t)
+            if t0 == 2:
+                add_up(z, 0)
+                add_up(z, 1)
+        add_up(z, 2)
+        add_up(z, 3)
+        head_out(y)
+        pool_gain(z)
+        pool_turn(z)
+        pool_quant(z)
+        head_out(z)

from contextlib import ExitStack

import concourse.mybir as mybir
from concourse.masks import make_identity

B, F, D, A, O = 512, 8, 512, 512, 1024
FLOPS = 2 * B * 28 * D * A + 2 * B * D * O

F32 = mybir.dt.float32
BF16 = mybir.dt.bfloat16
U32 = mybir.dt.uint32
U8 = mybir.dt.uint8
E4M3 = mybir.dt.float8_e4m3fn
FP8X4 = mybir.dt.float8_e4m3fn_x4
MULT = mybir.AluOpType.mult
ADD = mybir.AluOpType.add
SUB = mybir.AluOpType.subtract
MAX = mybir.AluOpType.max
MIN = mybir.AluOpType.min
ACT = mybir.ActivationFunctionType
AX = mybir.AxisListType

P = 128
NBT = B // P
FI = F - 1
CHUNKS = [
    ([(0, 1, 2)], [(0, 3, 2)]),
    ([(0, 5, 3)], [(1, 2, 1)]),
    ([(1, 3, 2)], [(1, 5, 2)]),
    ([(1, 7, 1)], [(2, 3, 3)]),
    ([(2, 6, 2)], [(3, 4, 2)]),
    ([(3, 6, 2)], [(4, 5, 2)]),
    ([(4, 7, 1)], [(5, 6, 2), (6, 7, 1)]),
]
NCH = len(CHUNKS)
NSLOT = NBT * NCH
MASKED = float(2.0 ** 100)
VEC2 = (3,)
SV = (0, 2, 3, 5,)
LE = 3
LQ = 1
LU = 1
TO = 0
WK = [(3, 4, 5, 6, 7, 8, 9, 10), (3, 4, 5, 6, 7, 8, 9, 9), (3, 3, 4, 4, 5, 5, 6, 6)]
SGS = (1, 2, 3, 4,)
SPLIT = True
MXB = 3
UTB = 2
ORDER = "pq h3 mask z0 q v z1 z2 sum z3 u sb pt w0 ho e0 h add sc out se gs sv sd gn d0 d1 spb o0 sa w1 e1 pg o1 g t".split()


def tile_afmpairattentionpooling_kernel(tc, v, ga, wa, ba, h, gp, wp_bytes, wp_scale, out):
    nc = tc.nc
    with ExitStack() as ctx:
        keep = ctx.enter_context(tc.tile_pool(name="keep", bufs=1))
        work = ctx.enter_context(tc.tile_pool(name="work", bufs=2))
        psum = ctx.enter_context(tc.psum_pool(name="psum", bufs=1))
        ctx.enter_context(nc.allow_non_contiguous_dma(reason="vectors of 512 onto the partitions"))
        ctx.enter_context(tc.manual_schedule())

        vn, vd, vT, vg, vgp, eg, codes, planes = {}, {}, {}, {}, {}, {}, {}, {}
        zt, mxs, ut, pe, den, mn, inv, hl, xb, am, wt, qt, pn = {}, {}, {}, {}, {}, {}, {}, {}, {}, {}, {}, {}, {}
        pool_n, pool_b, pool_c, pool_s, turned = {}, {}, {}, {}, {}

        idb = keep.tile([P, P], BF16, name="idb")
        id32 = keep.tile([P, P], F32, name="id32")
        make_identity(nc, idb[:])
        make_identity(nc, id32[:])
        neg = []
        for n in range(2):
            t = keep.tile([P, FI, F], F32, name="neg%d" % n)
            for i in range(FI):
                nc.gpsimd.memset(t[:, i, 0 : i + 1], MASKED)
            neg.append(t)
        junk = []
        for n in range(4):
            t = keep.tile([P, P], BF16, name="junk%d" % n)
            junk.append(t)

        def load_v(b, pieces):
            vn[b] = work.tile([P, F, D], BF16, name="vn", tag="vn", bufs=2)
            for f0, f1 in pieces:
                nc.sync.dma_start(out=vn[b][:, f0:f1, :], in_=v[b * P : (b + 1) * P, f0:f1, :])

        def load_vd(b):
            vd[b] = work.tile([P, 16, D], BF16, name="vd", tag="vd", bufs=2)
            src = v[b * P : (b + 1) * P].rearrange("(g r) j k -> (r j) g k", r=8)
            for hh in range(2):
                nc.sync.dma_start(out=vd[b][64 * hh : 64 * hh + 64], in_=src)

        ga_b = keep.tile([P, 4], BF16, name="ga_b")
        nc.sync.dma_start(out=ga_b[:], in_=ga.rearrange("(p t) -> p t", t=4))
        load_v(0, [(0, 2), (2, 4), (4, 6)])
        wa_raw = keep.tile([P, 4, A], BF16, name="wa_raw")
        nc.sync.dma_start(out=wa_raw[:], in_=wa.rearrange("(p j) a -> p j a", j=4))
        nc.sync.dma_start(out=vn[0][:, 6:8, :], in_=v[0:P, 6:8, :])
        ba_b = keep.tile([P, 4, 2], BF16, name="ba_b")
        nc.sync.dma_start(out=ba_b[:, :, 0], in_=ba.rearrange("(c p) -> p c", p=P))
        h_b = keep.tile([P, 4, 2], BF16, name="h_b")
        nc.sync.dma_start(out=h_b[:, :, 0], in_=h.rearrange("(c p) -> p c", p=P))
        wps = keep.tile([P, 4], F32, name="wps")
        nc.sync.dma_start(out=wps[:], in_=wp_scale.rearrange("(p t) o -> p (t o)", t=4))
        wpb = keep.tile([P, 4, O], U8, name="wpb")
        nc.sync.dma_start(out=wpb[:], in_=wp_bytes.rearrange("(p t) o -> p t o", t=4))
        load_v(1, [(0, 8)])
        gp_r = keep.tile([P, D], BF16, name="gp_r")
        nc.sync.dma_start(out=gp_r[:], in_=gp.partition_broadcast(P))
        load_vd(0)
        load_vd(1)

        def turn(b, m):
            if m == 0:
                vT[b] = work.tile([P, F, P, 4], BF16, name="vT", tag="vT", bufs=4, align_bytes=64)
            if b == 0:
                tp = psum.tile([P, 2, 2, P], F32, name="tp", tag="mx", bufs=MXB)
            else:
                tp = psum.tile([P, 2, 2, P], F32, name="tp", tag="tp", bufs=1)
            words = vn[b][:].bitcast(F32)
            for f in range(2):
                for u in range(2):
                    src = words[:, 2 * m + f, :].rearrange("r (w u) -> r u w", u=2)[:, u, :]
                    nc.tensor.transpose(tp[:, f, u, :], src, id32[:])
            return tp

        def turn_out(b, m, tp, eng):
            dst = vT[b][:, 2 * m : 2 * m + 2].bitcast(F32)
            src = tp[:].rearrange("p f u b -> p f b u")
            if eng == 0:
                nc.scalar.copy(out=dst, in_=src)
            else:
                nc.vector.tensor_copy(out=dst, in_=src)

        def on_pe(b):
            return 4 if b == 0 else 5

        def gains(b):
            i0 = on_pe(b)
            vg[b] = work.tile([P, 3, P, 4], F32, name="vg", tag="vg", bufs=2, align_bytes=64)
            nc.vector.tensor_tensor(
                out=vg[b][:, 0 : FI - i0],
                in0=vT[b][:, i0:FI],
                in1=ga_b[:].unsqueeze(1).unsqueeze(1).to_broadcast([P, FI - i0, P, 4]),
                op=MULT,
            )

        def gain_pe(b, i):
            if i >= on_pe(b) or (b, i) in vgp:
                return
            vgp[b, i] = psum.tile([P, P, 4], F32, name="vgp", tag="vgp", bufs=1)
            for t in range(4):
                nc.tensor.matmul(
                    out=vgp[b, i][:, :, t], lhsT=dg[t][:], rhs=vT[b][:, i, :, t], start=True, stop=True
                )

        def products(s, part):
            b, c = divmod(s, NCH)
            if part == 0:
                eg[s] = work.tile([P, 4, P, 4], BF16, name="eg", tag="eg", bufs=4, align_bytes=64)
            o = 0 if part == 0 else sum(n for i, j0, n in CHUNKS[c][0])
            for i, j0, n in CHUNKS[c][part]:
                if i < on_pe(b):
                    left = vgp[b, i][:]
                else:
                    left = vg[b][:, i - on_pe(b)]
                nc.vector.tensor_tensor(
                    out=eg[s][:, o : o + n],
                    in0=left.unsqueeze(1).to_broadcast([P, n, P, 4]),
                    in1=vT[b][:, j0 : j0 + n],
                    op=MULT,
                )
                o += n

        def quantize(s):
            codes[s] = work.tile([P, 512], U32, name="codes", tag="codes", bufs=3, align_bytes=64)
            planes[s] = work.tile([P, 512], U8, name="planes", tag="planes", bufs=3, align_bytes=64)
            nc.vector.quantize_mx(
                out=codes[s][:].bitcast(FP8X4), scales=planes[s][:], in_=eg[s][:].rearrange("p q b t -> p (q b t)")
            )

        def hidden(s, blocks):
            if 0 in blocks:
                zt[s] = work.tile([P, 4, 512], F32, name="zt", tag="zt", bufs=3)
            for a in blocks:
                mxs[s, a] = psum.tile([P, 512], F32, name="mx", tag="mx", bufs=MXB)
                nc.tensor.matmul_mx(
                    out=mxs[s, a][:],
                    lhsT=wa_codes[:, a * P : (a + 1) * P].bitcast(FP8X4),
                    lhsT_scale=wa_planes[:, a * P : (a + 1) * P],
                    rhs=codes[s][:].bitcast(FP8X4),
                    rhs_scale=planes[s][:],
                    start=True,
                    stop=True,
                )

        def on_vector(s, a):
            return a == 3 and s % NCH in VEC2

        def sign_on_vector(s, a):
            return a == 0 and s % NCH in SV

        def relu_s(s, blocks):
            for a in blocks:
                if not on_vector(s, a):
                    nc.scalar.activation(
                        out=zt[s][:, a, :], in_=mxs[s, a][:], func=ACT.Relu, bias=ba_f[:, a : a + 1], scale=1.0
                    )

        def weigh_g(s):
            for a in range(4):
                if not on_vector(s, a) and not sign_on_vector(s, a) and not sign_on_scalar(s, a):
                    nc.gpsimd.tensor_scalar(
                        out=zt[s][:, a, :], in0=zt[s][:, a, :], scalar1=h_f[:, a : a + 1], scalar2=nhba[:, a : a + 1],
                        op0=MULT, op1=ADD,
                    )

        def sign_on_scalar(s, a):
            return a == 1 and s % NCH in SGS

        def sign_s(s):
            for a in range(4):
                if sign_on_scalar(s, a):
                    nc.scalar.activation(
                        out=zt[s][:, a, :], in_=zt[s][:, a, :], func=ACT.Identity, bias=nhba[:, a : a + 1],
                        scale=h_f[:, a : a + 1],
                    )

        def sign_v(s):
            for a in range(4):
                if sign_on_vector(s, a):
                    nc.vector.tensor_scalar(
                        out=zt[s][:, a, :], in0=zt[s][:, a, :], scalar1=h_f[:, a : a + 1], scalar2=nhba[:, a : a + 1],
                        op0=MULT, op1=ADD,
                    )

        def weigh_v(s):
            for a in range(4):
                if on_vector(s, a):
                    nc.vector.tensor_scalar(
                        out=zt[s][:, a, :], in0=mxs[s, a][:], scalar1=nba[:, a : a + 1], scalar2=h_f[:, a : a + 1],
                        op0=MAX, op1=MULT,
                    )

        def scores(s):
            ut[s] = psum.tile([P, 4, P], F32, name="ut", tag="ut", bufs=UTB)
            for q in range(4):
                for a in range(4):
                    nc.tensor.matmul(
                        out=ut[s][:, q, :],
                        lhsT=zt[s][:, a, q * P : (q + 1) * P],
                        rhs=id32[:],
                        start=(a == 0),
                        stop=(a == 3),
                        is_transpose=True,
                    )

        def sums(s):
            b, c = divmod(s, NCH)
            q = 0
            for part in range(2):
                for i, j0, n in CHUNKS[c][part]:
                    for j in range(j0, j0 + n):
                        nc.scalar.activation(
                            out=junk[q][:], in_=ut[s][:, q, :], func=ACT.Copy, scale=-1.0,
                            accum_out=neg[b % 2][:, i, j : j + 1],
                        )
                        q += 1

        def soft_b(b):
            mn[b] = work.tile([P, 1], F32, name="mn", tag="mn")
            nc.vector.tensor_reduce(out=mn[b][:], in_=neg[b % 2][:].rearrange("p i j -> p (i j)"), axis=AX.X, op=MIN)

        def soft_c(b):
            pe[b] = work.tile([P, FI, F], F32, name="pe", tag="pe")
            den[b] = work.tile([P, 1], F32, name="den", tag="den")
            nc.scalar.activation(
                out=pe[b][:], in_=neg[b % 2][:], func=ACT.Exp, bias=mn[b][:], scale=-1.0, accum_out=den[b][:]
            )

        def soft_d(b):
            hl[b] = work.tile([P, FI, 2, F], BF16, name="hl", tag="hl")
            nc.vector.tensor_copy(out=hl[b][:, :, 0, :], in_=pe[b][:])
            nc.vector.tensor_tensor(out=hl[b][:, :, 1, :], in0=pe[b][:], in1=hl[b][:, :, 0, :], op=SUB)

        def soft_e(b):
            inv[b] = work.tile([P, 1], F32, name="inv", tag="inv", bufs=4)
            nc.vector.reciprocal(out=inv[b][:], in_=den[b][:])

        def spread_a(b):
            xb[b] = work.tile([P, FI * 2, 8, F], BF16, name="xb", tag="xb", bufs=1)
            src = hl[b][:].rearrange("p i h j -> p (i h) j").unsqueeze(2).to_broadcast([P, FI * 2, 8, F])
            nc.scalar.copy(out=xb[b][:], in_=src)

        def spread_b(b):
            tp = psum.tile([P, FI, P], BF16, name="tpb", tag="wt" if b == NBT - 1 else "tp", bufs=1)
            flat = xb[b][:].rearrange("p x r j -> p (x r j)")
            for i in range(FI):
                nc.tensor.transpose(tp[:, i, :], flat[:, i * P : (i + 1) * P], idb[:])
            return tp

        def spread_c(b, tp):
            am[b] = work.tile([P, 16, FI, 8], BF16, name="am", tag="am", bufs=3)
            nc.vector.tensor_tensor(
                out=am[b][:].rearrange("m g i r -> m i g r"),
                in0=tp[:].rearrange("m i (g r) -> m i g r", r=8),
                in1=mask[:].unsqueeze(1).unsqueeze(1).to_broadcast([P, FI, 16, 8]),
                op=MULT,
            )

        def weigh(b, hh, t):
            if b == NBT - 1:
                wt[b, hh, t] = psum.tile([P, FI, 64], F32, name="wt", tag="mx", bufs=MXB)
            else:
                wt[b, hh, t] = psum.tile([P, FI, 64], F32, name="wt", tag="wt", bufs=1)
            for g in range(8):
                nc.tensor.matmul(
                    out=wt[b, hh, t][:, :, 8 * g : 8 * g + 8],
                    lhsT=vd[b][:, 8 * hh + g, :].rearrange("m (p t) -> m t p", t=4)[:, t, :],
                    rhs=am[b][:, 8 * hh + g],
                    start=True,
                    stop=True,
                )

        def weigh_out(b, hh, t):
            if b not in qt:
                qt[b] = work.tile([P, 4, FI, P], F32, name="qt", tag="qt", bufs=2)
            cols = slice(64 * hh, 64 * hh + 64)
            nc.vector.tensor_tensor(
                out=qt[b][:, t, :, cols], in0=wt[b, hh, t][:], in1=vT[b][:, 0:FI, cols, t], op=MULT
            )

        def add_up(b, t):
            if t == 0:
                pn[b] = psum.tile([P, 4, P], F32, name="pn", tag="tp", bufs=1)
            for i in range(FI):
                nc.tensor.matmul(
                    out=pn[b][:, t, :], lhsT=qt[b][:, t, i, :], rhs=id32[:], start=(i == 0), stop=(i == FI - 1),
                    is_transpose=True,
                )

        def pool_gain(b):
            pool_n[b] = work.tile([P, P, 4], BF16, name="pool_n", tag="pool_n")
            nc.vector.scalar_tensor_tensor(
                out=pool_n[b][:],
                in0=pn[b][:].rearrange("b t p -> b p t"),
                scalar=inv[b][:],
                in1=gp_r[:].rearrange("b (p t) -> b p t", t=4),
                op0=MULT,
                op1=MULT,
            )

        def pool_turn(b):
            tp = psum.tile([P, 2, P], F32, name="tpp", tag="tp", bufs=1)
            words = pool_n[b][:].rearrange("b p t -> b (p t)").bitcast(F32).rearrange("b (w u) -> b u w", u=2)
            for u in range(2):
                nc.tensor.transpose(tp[:, u, :], words[:, u, :], id32[:])
            pool_b[b] = work.tile([P, P, 4], BF16, name="pool_b", tag="pool_b", align_bytes=64)
            nc.scalar.copy(out=pool_b[b][:].bitcast(F32), in_=tp[:].rearrange("p u b -> p b u"))

        def pool_quant(b):
            pool_c[b] = work.tile([P, P], U32, name="pool_c", tag="pool_c", align_bytes=64)
            pool_s[b] = work.tile([P, P], U8, name="pool_s", tag="pool_s", align_bytes=64)
            nc.vector.quantize_mx(
                out=pool_c[b][:].bitcast(FP8X4), scales=pool_s[b][:], in_=pool_b[b][:].rearrange("p b t -> p (b t)")
            )

        def head_out(b):
            osb = work.tile([P, O], F32, name="osb", tag="osb", bufs=2)
            for n in range(2):
                cols = slice(512 * n, 512 * n + 512)
                mx = psum.tile([P, 512], F32, name="mxo", tag="mx", bufs=MXB)
                nc.tensor.matmul_mx(
                    out=mx[:],
                    lhsT=pool_c[b][:].bitcast(FP8X4),
                    lhsT_scale=pool_s[b][:],
                    rhs=wp_codes[:, cols].bitcast(FP8X4),
                    rhs_scale=wp_planes[:, cols],
                    start=True,
                    stop=True,
                )
                if b == NBT - 1 and n == 1:
                    nc.vector.tensor_copy(out=osb[:, cols], in_=mx[:])
                else:
                    nc.scalar.copy(out=osb[:, cols], in_=mx[:])
                nc.sync.dma_start(out=out[b * P : (b + 1) * P, cols], in_=osb[:, cols])

        dg = []
        for t in range(4):
            d = keep.tile([P, P], BF16, name="dg%d" % t)
            nc.vector.tensor_scalar(out=d[:], in0=idb[:], scalar1=ga_b[:, t : t + 1], scalar2=None, op0=MULT)
            dg.append(d)
        wa_g = keep.tile([P, A, 4], BF16, name="wa_g", align_bytes=64)
        tp0 = turn(0, 0)
        tp1 = turn(0, 1)
        tp2 = turn(0, 2)
        turn_out(0, 0, tp0, 0)
        turn_out(0, 1, tp1, 1)
        turn_out(0, 2, tp2, 0)
        gain_pe(0, 0)
        products(0, 0)
        for n in range(2):
            dst = wa_g[:, 256 * n : 256 * n + 256, :]
            wsrc = wa_raw[:, :, 256 * n : 256 * n + 256].rearrange("p j a -> p a j")
            if n == 0:
                nc.scalar.copy(out=dst, in_=wsrc)
            else:
                nc.gpsimd.tensor_scalar(out=dst, in0=wsrc, scalar1=1.0, scalar2=0.0, op0=MULT, op1=ADD)
        products(0, 1)
        tp3 = turn(0, 3)
        turn_out(0, 3, tp3, 0)
        wa_codes = keep.tile([P, A], U32, name="wa_codes", align_bytes=64)
        wa_planes = keep.tile([P, A], U8, name="wa_planes", align_bytes=64)
        nc.vector.quantize_mx(
            out=wa_codes[:].bitcast(FP8X4), scales=wa_planes[:], in_=wa_g[:].rearrange("p a j -> p (a j)")
        )
        quantize(0)
        products(1, 0)
        mask = keep.tile([P, 8], BF16, name="mask")
        ba_f = keep.tile([P, 4], F32, name="ba_f")
        nc.gpsimd.tensor_copy(out=ba_f[:], in_=ba_b[:, :, 0])
        h_f = keep.tile([P, 4], F32, name="h_f")
        nc.gpsimd.tensor_copy(out=h_f[:], in_=h_b[:, :, 0])
        nba = keep.tile([P, 4], F32, name="nba")
        nc.gpsimd.tensor_scalar(out=nba[:], in0=ba_f[:], scalar1=-1.0, scalar2=None, op0=MULT)
        nhba = keep.tile([P, 4], F32, name="nhba")
        nc.gpsimd.tensor_tensor(out=nhba[:], in0=h_f[:], in1=nba[:], op=MULT)
        hidden(0, (0, 1, 2) if SPLIT else (0, 1, 2, 3))
        gain_pe(0, 1)
        products(1, 1)
        gain_pe(0, 1)
        products(2, 0)
        products(2, 1)
        with nc.allow_low_precision(reason="sums of zeros and a single one"):
            nc.vector.tensor_reduce(
                out=mask[:], in_=idb[:].rearrange("p (h r j) -> p r h j", h=2, r=8), axis=AX.XY, op=ADD
            )

        wpl = keep.tile([P, 4, O], BF16, name="wpl")
        wpg = keep.tile([P, O, 4], BF16, name="wpg", align_bytes=64)
        wp_codes = keep.tile([P, O], U32, name="wp_codes", align_bytes=64)
        wp_planes = keep.tile([P, O], U8, name="wp_planes", align_bytes=64)

        def widen(t):
            nc.scalar.activation(
                out=wpl[:, t, :], in_=wpb[:, t, :].bitcast(E4M3), func=ACT.Copy, scale=wps[:, t : t + 1]
            )

        widen(0)
        widen(1)

        for s in range(NSLOT):
            b, c = divmod(s, NCH)
            live = s < NSLOT
            off = {}
            for bb in range(NBT):
                k = s - NCH * (bb + 1) - (LU - 1)
                if 0 <= k <= 12:
                    off[k] = bb
            wi = []
            ta = []
            for bb in range(NBT - 1):
                k = s - NCH * (bb + 1) - (LU - 1)
                for n in range(8):
                    if k == WK[bb][n]:
                        wi.append((bb, n % 2, n // 2))
                if k == WK[bb][7] + 1:
                    ta.append(bb)

            def z_rest():
                relu_s(s, (1, 2, 3))

            def tout():
                if live and b + 1 < NBT and 1 <= c - TO <= 4:
                    turn_out(b + 1, c - TO - 1, turned[b + 1, c - TO - 1], 0)

            def gpe(n, part):
                if s + n < NSLOT:
                    for i, j0, m in CHUNKS[(s + n) % NCH][part]:
                        gain_pe((s + n) // NCH, i)

            def each(ts, f):
                for t in ts:
                    f(t)

            def at(k, f, last=False):
                if k in off and (last or off[k] < NBT - 1):
                    f(off[k])

            def stage(n, f):
                for bb in range(NBT - 1):
                    if s - NCH * (bb + 1) - (LU - 1) == n + WK[bb][7] + 1:
                        f(bb)

            def spb(z):
                turned[z] = spread_b(z)

            def trn():
                if live and b + 1 < NBT and 0 <= c - TO <= 3:
                    turned[b + 1, c - TO] = turn(b + 1, c - TO)

            items = {
                "q": lambda: quantize(s + LQ) if s + LQ < NSLOT else None,
                "e0": lambda: products(s + LE, 0) if s + LE < NSLOT else None,
                "e1": lambda: products(s + LE, 1) if s + LE < NSLOT else None,
                "z0": lambda: relu_s(s, (0,)) if live else None,
                "z1": lambda: relu_s(s, (1,)) if live else None,
                "z2": lambda: relu_s(s, (2,)) if live else None,
                "z3": lambda: relu_s(s, (3,)) if live else None,
                "g": lambda: weigh_g(s) if live else None,
                "gs": lambda: sign_s(s) if live else None,
                "v": lambda: weigh_v(s) if live else None,
                "h3": lambda: hidden(s, (3,)) if live and SPLIT else None,
                "h": lambda: hidden(s + 1, (0, 1, 2) if SPLIT else (0, 1, 2, 3)) if s + 1 < NSLOT else None,
                "sum": lambda: sums(s - LU - 1) if 0 <= s - LU - 1 < NSLOT else None,
                "out": tout,
                "sb": lambda: at(1, soft_b, True),
                "sc": lambda: at(1, soft_c, True),
                "sd": lambda: at(1, soft_d, True),
                "sa": lambda: at(1, spread_a, True),
                "se": lambda: at(1, soft_e, True),
                "mask": lambda: at(3, lambda z: spread_c(z, turned[z]), True),
                "u": lambda: scores(s - LU) if 0 <= s - LU < NSLOT else None,
                "w0": lambda: each(wi[0:1], lambda z: weigh(*z)),
                "o0": lambda: each(wi[0:1], lambda z: weigh_out(*z)),
                "w1": lambda: each(wi[1:2], lambda z: weigh(*z)),
                "o1": lambda: each(wi[1:2], lambda z: weigh_out(*z)),
                "d1": lambda: gpe(LE, 1),
                "d0": lambda: gpe(LE + 1, 0),
                "sv": lambda: sign_v(s) if live else None,
                "add": lambda: each(ta, lambda z: each(range(4), lambda t: add_up(z, t))),
                "pg": lambda: stage(0, pool_gain),
                "pt": lambda: stage(1, pool_turn),
                "pq": lambda: stage(2, pool_quant),
                "ho": lambda: stage(2, head_out),
                "spb": lambda: at(2, spb, True),
                "gn": lambda: gains(b) if live and c == 1 else None,
                "t": trn,
            }
            for name in ORDER:
                items[name]()
            if s == 0:
                load_v(2, [(0, 8)])
            if s == 4:
                load_v(3, [(0, 8)])
            if s == 18:
                load_vd(2)
            if s == 25:
                load_vd(3)
            if s in (0, 1):
                widen(s + 2)
            if 7 <= s < 11:
                n0 = 256 * (s - 7)
                nc.scalar.copy(
                    out=wpg[:, n0 : n0 + 256, :], in_=wpl[:, :, n0 : n0 + 256].rearrange("p j n -> p n j")
                )
            if s == 12:
                nc.vector.quantize_mx(
                    out=wp_codes[:].bitcast(FP8X4), scales=wp_planes[:], in_=wpg[:].rearrange("p n j -> p (n j)")
                )

        y, z = NBT - 2, NBT - 1
        sums(NSLOT - 2)
        scores(NSLOT - 1)
        for t in range(4):
            add_up(y, t)
        sums(NSLOT - 1)
        soft_b(z)
        soft_c(z)
        soft_d(z)
        spread_a(z)
        pool_gain(y)
        soft_e(z)
        tp = spread_b(z)
        pool_turn(y)
        spread_c(z, tp)
        pool_quant(y)
        for t0 in (0, 2):
            for hh in range(2):
                for t in (t0, t0 + 1):
                    weigh(z, hh, t)
                    weigh_out(z, hh, t)
            if t0 == 2:
                add_up(z, 0)
                add_up(z, 1)
        add_up(z, 2)
        add_up(z, 3)
        head_out(y)
        pool_gain(z)
        pool_turn(z)
        pool_quant(z)
        head_out(z)
